import numpy as np, ml_dtypes
CORES = [1,5,17,21,33,37,49,53]
N = 8
import mx_ref
BF = ml_dtypes.bfloat16
def gentries(a):
    return np.ascontiguousarray(a.reshape(8, 16, -1).transpose(0, 2, 1)).reshape(8, -1)
def gtable(e):
    e = np.asarray(e); return np.ascontiguousarray(e.reshape(8, -1, 16).transpose(0, 2, 1)).reshape(128, -1).astype(np.int32)
def gcols(t, e):
    v = np.concatenate([t.reshape(8, 16, -1, 4), np.zeros((8, 16, 1, 4), BF)], axis=2)
    return np.ascontiguousarray(np.stack([v[g][:, e[g]] for g in range(8)])).reshape(128, -1)
def gpick(z, e):
    return np.concatenate([z[16 * g:16 * g + 16][:, e[g]] for g in range(8)])
def tile(rs):
    return np.stack(rs, axis=2).reshape(128, -1).astype(BF)
def pick(q, e):
    c = np.concatenate([q[0].reshape(128, -1, 4), np.zeros((128, 1, 4), np.uint8)], axis=1); s = np.concatenate([q[1], np.ones((16, 1), np.uint8)], axis=1)
    return (np.ascontiguousarray(c[:, e].reshape(128, -1)), np.ascontiguousarray(s[:, e]))
def join(*qs):
    return (np.concatenate([q[0] for q in qs], axis=1), np.concatenate([q[1] for q in qs], axis=1))
def put(q, e, v):
    c, s = q[0].reshape(128, -1, 4).copy(), q[1].copy(); c[:, e] = v[0].reshape(128, -1, 4); s[:, e] = v[1]
    return (c.reshape(128, -1), s)
def pk(c, s):
    return (np.ascontiguousarray(c), mx_ref.live(s))
def emit(q):
    return q[0], q[1]
def packed(v, rng):
    q = [mx_ref.quantize(np.ascontiguousarray(v[r])) for r in range(N)]
    return np.stack([a for a, b in q]), np.stack([mx_ref.plane(b, rng) for a, b in q])
def values_of_codes():
    e, c = np.zeros((128, 128, 4), np.float32), np.zeros((128, 2, 4), np.uint8)
    e[np.arange(128), np.arange(128), 0] = 1
    c[:127, :, 0] = np.arange(256).reshape(2, 128).T[:127]
    return mx_ref.matmul(mx_ref.quantize(e.reshape(128, 512).astype(BF)), (c.reshape(128, 8), np.full((16, 2), 127, np.uint8))).T.reshape(-1).astype(np.float64)
CODE_VALUE, SCALE_VALUE = values_of_codes(), 2.0 ** (np.arange(256) - 127.0)
def decode(q):
    return (CODE_VALUE[q[0]].reshape(16, 8, -1, 4) * SCALE_VALUE[q[1]][:, None, :, None] + 0.0).reshape(128, -1).astype(np.float32)
def f(rng, *shape):
    return mx_ref.flush((rng.standard_normal(shape, dtype=np.float32) * np.exp2(rng.integers(-2, 3, shape[:-1] + (1,)))).astype(BF))
def wide(rng, *shape, cols=0):
    v = rng.standard_normal(shape, dtype=np.float32) * np.exp2(rng.integers(-12, 13, shape)).astype(np.float32)
    if cols: v *= np.repeat(np.exp2(rng.integers(-cols, cols + 1, shape[:-2] + (1, shape[-1] // 4))) * (rng.random(shape[:-2] + (1, shape[-1] // 4)) > 0.0625), 4, axis=-1).astype(np.float32)
    return mx_ref.flush(v.astype(BF))
C = 256
MASK = [1, 2, 4]
PARITY = np.array([(r ^ (r >> 1) ^ (r >> 2)) & 1 for r in range(N)])
def numbers_of(rng):
    return {"x": np.array(f(rng, N, 128, 4 * C)), "u": np.array(f(rng, N, 128, 512)), "v": np.array(f(rng, N, 128, 512))}
def stored(k):
    return {"fl": np.stack([gtable(k[r]) for r in range(N)])}
def lists(rng):
    return stored(rng.permuted(np.tile(np.arange(C), (N, 8, 1)), axis=2))
def layers(rng):
    return np.array(f(rng, N, 128, 2048)).reshape(N, 8, 16, 4, 8, 16, 4)
def weights(rng, w):
    c, p = packed(np.ascontiguousarray(w).reshape(N, 128, 2048), rng)
    return {"wc": c, "ws": p}
def setup_inputs(rng):
    return {**numbers_of(rng), **lists(rng), **weights(rng, layers(rng))}
def setup_inputs_long(rng):
    d = numbers_of(rng)
    kind = rng.permutation(8)
    s = np.tile(rng.choice([-1.0, 1.0], (8, C)), (N, 1, 1))
    k = np.zeros((N, 8, C), np.int64)
    for g in range(8):
        c, p = rng.permutation(C), int(rng.integers(C))
        if kind[g] == 0: c, p = np.arange(C), C - N // 2
        if kind[g] == 1: c = np.arange(C)[::-1]
        k[:, g, c] = np.roll(c, -1)
        for r in range(N):
            if kind[g] in (0, 1, 3, 4): s[r, g, c[(p + r) % C]] *= -1
            if kind[g] == 2 and PARITY[r]: s[r, g, c[p]] *= -1
            if kind[g] == 6 and PARITY[r]: s[r, g] *= -1
            if kind[g] == 7:
                s[r, g] = rng.choice([-1.0, 1.0], C)
                k[r, g] = np.arange(C)
    x = d["x"].reshape(N, 8, 16, C, 4)
    x[:, :, 0] = 0
    x[:, :, 0, :, 0] = s.astype(np.float32).astype(BF)
    u = d["u"].reshape(N, 128, 128, 4)
    u[:, :, ::16] = 0
    for h in range(0, 128, 16): u[:, h, h, 0] = 1
    w = layers(rng)
    w[:, :, :, :, :, 0] = 0
    return {"x": x.reshape(N, 128, 4 * C), "u": u.reshape(N, 128, 512), "v": d["v"], **stored(k), **weights(rng, w)}
def setup_inputs_near(rng):
    d = numbers_of(rng)
    o, e = rng.permutation(N) % 2, rng.permutation(N)
    k = np.where(o == 0, 2.0 ** -27, 1.0)
    m = np.where(o == 0, 2.0 ** -30, 1.0)
    s = rng.integers(-1, 2, (N, 8, C))
    s[e[0]] = 0
    s[e[1]] = 1
    x = d["x"].astype(np.float32).reshape(N, 8, 16, C, 4)
    x[o == 0] = 0
    x[:, :, :3] = 0
    x[:, :, 8:] = 0
    x[:, :, 0, :, 0] = np.where(s == 0, 1.0, 1.125 * s) * k[:, None, None]
    x[:, :, 1, :, 0] = np.where(s == 0, -1.125, -1.25 * s) * k[:, None, None]
    x[:, :, 3, :, 0] = k[:, None, None]
    x[:, :, 8, :, 0] = rng.choice([-1.0, 1.0], (N, 8, C)) * 2.0 ** -30
    x[:, :, 9, :, 0] = 2.0 ** -26
    for r in range(N):
        for g in rng.permutation(8)[:4]: x[r, g, 0, rng.integers(C), 0] = 2.0 ** 30 * rng.choice([-1.0, 1.0])
    u = d["u"].reshape(N, 128, 128, 4)
    u[:, :, ::16] = 0
    for h in range(0, 128, 16):
        u[:, h, h, 0] = (1.125 * m).astype(np.float32).astype(BF)
        u[:, h + 1, h, 0] = m.astype(np.float32).astype(BF)
        u[:, h + 2, h, 0] = m.astype(np.float32).astype(BF)
    w = layers(rng)
    w[:, :, :, :, :, :10] = 0
    for g in range(8): w[:, g, 8, 0, g, 2, 0] = 2.0 ** -7
    return {"x": x.reshape(N, 128, 4 * C).astype(BF), "u": u.reshape(N, 128, 512), "v": d["v"], **lists(rng), **weights(rng, w)}
def setup_inputs_odd(rng):
    d = numbers_of(rng)
    e = (PARITY[:, None] + rng.permutation(8)) % 2
    a = 1.0 + (2 * rng.integers(0, 64, (N, 8, 16, C, 4)) + 1) * 2.0 ** -7
    x = np.zeros((N, 8, 16, C, 4))
    x[:, :, :8] = a[:, :, :8] * np.exp2(-rng.integers(0, 7, (N, 8, 8, C, 4)).astype(np.float64)) * rng.choice([-1.0, 1.0], (N, 8, 8, C, 4))
    x[:, :, 0] = 0
    x[:, :, 0, :, 0] = 1.96875 * 2.0 ** 8 * rng.choice([-1.0, 1.0], (N, 8, C))
    x[:, :, 8:] = np.where(e[:, :, None, None, None] == 0, a[:, :, 8:] * np.exp2(12.0 - rng.integers(8, 15, (N, 8, 8, C, 4))), 0.0)
    x[:, :, 8, :, 0] = (np.where(e == 0, -1.0, 1.0) * 1.96875 * 2.0 ** 12)[:, :, None]
    u = d["u"].reshape(N, 128, 128, 4)
    u[:, 8::16, ::16] = 0
    w = layers(rng)
    for i in (0, 8):
        w[:, :, i] = 0
        w[:, :, :, :, :, i] = 0
    for g in rng.permutation(8)[:4]:
        x[:, g, :3] = 0
        x[:, g, 0, :, 0] = 1.96875 * 2.0 ** 8
        x[:, g, 1, :, 0] = (8 + rng.integers(-1, 2, (N, C))) * 2.0 ** -8
        x[:, g, 2, :, 0] = -2.0 ** -5
        x[:, g, 8:] = 0
        x[:, g, 8, :, 0] = 1.96875 * 2.0 ** 12
        x[:, g, 9] = rng.integers(1, 16, (N, C, 4)) * 2.0 ** -4
        u[:, 16 * g, ::16] = 0
        u[:, :, 16 * g] = 0
        u[:, 16 * g + 1:16 * g + 3, 16 * g, 0] = 1
        w[:, :, :, :, g] = 0
        for i in (0, 8): w[:, g, i, 0, g, i, 0] = -0.5
        for b in range(4): w[:, g, 9, b, g, 10, b] = 256.0
    return {"x": x.astype(np.float32).reshape(N, 128, 4 * C).astype(BF), "u": u.reshape(N, 128, 512), "v": d["v"], **lists(rng), **weights(rng, w)}
def setup_inputs_ends(rng):
    d = numbers_of(rng)
    x = np.zeros((N, 8, 16, C, 4))
    u = d["u"].astype(np.float32).reshape(N, 128, 128, 4)
    v = np.zeros((N, 128, 512))
    w = np.zeros((N, 128, 4, 128, 4), np.float32)
    o = rng.permutation(N) % 4
    third, others = np.flatnonzero(o == 2), np.flatnonzero(o != 2)
    if len(third) == 2 and third[0] ^ third[1] == MASK[0]:
        p = rng.choice(others)
        o[third[1]] = o[p]
        o[p] = 2
    i, at = np.arange(128), np.arange(C)
    k = np.zeros((N, 8, C), np.int64)
    for r in range(N):
        h = rng.permutation(8)
        c = np.where(h < 2, 0.0, h % 2 * 2.0 - 1.0)[None, :, None]
        low = -(0.9 + 0.1 * rng.random((8, 16, C, 4))) * 2.0 ** 30
        if o[r] == 0: x[r] = low
        if o[r] == 1: x[r] = low * rng.choice([-1.0, 1.0], C)[:, None]
        if o[r] == 2: x[r] = -(1.0 + 0.125 * rng.integers(0, 8, (8, 16, C, 4))) * 2.0 ** -30
        if o[r] == 3: x[r] = d["x"][r].astype(np.float32).reshape(8, 16, C, 4)[:, :, :1]
        if o[r] < 2:
            u[r, :, ::16] = c * (0.9 + 0.1 * rng.random((128, 8, 4))) * 2.0 ** 30
            v[r] = rng.choice([-1.0, 1.0], (128, 512)) * (0.9 + 0.1 * rng.random((128, 512))) * 2.0 ** 30
        else: v[r] = rng.choice([-1.0, 1.0], (128, 512)) * (1.0 + 0.125 * rng.integers(0, 8, (128, 512))) * 2.0 ** -30
        if o[r] == 2: u[r, :, ::16] = c * (1.0 + 0.125 * rng.integers(0, 8, (128, 8, 4))) * 2.0 ** -30
        if o[r] == 3: u[r, :, ::16] *= np.abs(c).astype(np.float32)
        t = np.array([4.0, 8.0, 16.0])[rng.permutation(8) % 3]
        if o[r] == 2: t[:] = 2.0 ** -8
        if o[r] == 3: t[:] = 2.0 ** 5
        for b in range(4): w[r, i, b, i, b] = t[i // 16]
        for g, n in enumerate(rng.permutation(8) % 5): k[r, g] = [at, at[::-1], np.roll(at, -1), at ^ 1, rng.permutation(C)][n]
    return {"x": x.astype(np.float32).reshape(N, 128, 4 * C).astype(BF), "u": u.reshape(N, 128, 512).astype(BF), "v": v.astype(np.float32).astype(BF), **stored(k), **weights(rng, w.astype(BF))}
def setup_inputs_spread(rng):
    d = numbers_of(rng)
    w = layers(rng).reshape(N, 128, 4, 128, 4)
    i, r = np.arange(128), int(rng.integers(N))
    for b in range(4): w[r, i, b, i, b] = 256.0
    return {"x": wide(rng, N, 128, 4 * C, cols=6), "u": d["u"], "v": d["v"], **lists(rng), **weights(rng, w)}
def check_inputs(d):
    b = []
    for k in ("x", "u", "v"):
        a = np.abs(d[k].astype(np.float32))
        if not (np.isfinite(a).all() and ((a == 0) | (a >= 2.0 ** -30) & (a <= 2.0 ** 30)).all()): b.append("a value of " + k)
    none, least, most = [emit(mx_ref.quantize(np.full((128, 16), k, np.float32).astype(BF)))[1][0, 0] for k in (0.0, 2.0 ** -8, 2.0 ** 8)]
    for r in range(N):
        if not (np.sort(gentries(d["fl"][r]), axis=1) == np.arange(C)).all(): b.append("fl: a group's entries are no permutation")
        if ((d["wc"][r] == 0x7F) | (d["wc"][r] == 0xFF)).any(): b.append("wc: a code that is no number")
        s = mx_ref.live(d["ws"][r])
        if ((s != none) & ((s < least) | (s > most))).any(): b.append("ws: a scale out of range")
        if (((d["wc"][r].reshape(16, 8, 512, 4) & 0x7F) != 0) & (s == none)[:, None, :, None]).any(): b.append("wc: a code other than zero under the scale of zeros")
    return b
def returns(e, gate):
    at = np.tile(np.arange(C), (8, 1))
    step = np.where(gate, at, e)
    a = e
    for i in range(C): a = np.take_along_axis(step, a, axis=1)
    return np.where(gate, a, at)
def reference(x, u, v, fl, wc, ws):
    half = np.float32(0.5)
    qu = [mx_ref.quantize(u[r]) for r in range(N)]
    lay = [pk(wc[r], ws[r]) for r in range(N)]
    own = [gentries(fl[r]).astype(np.int64) for r in range(N)]
    now = [x[r] for r in range(N)]
    for m in MASK:
        q = [mx_ref.quantize(now[r]) for r in range(N)]
        t = [decode(q[r]) for r in range(N)]
        bit = [mx_ref.matmul(qu[r], q[r])[::16] > 0 for r in range(N)]
        made, new = [], []
        for r in range(N):
            d = r ^ m
            a = returns(own[d], bit[r] != bit[d])
            n = np.take_along_axis(own[r], a, axis=1)
            z = (gcols(t[r].astype(BF), n).astype(np.float32) + gcols(t[d].astype(BF), a).astype(np.float32)) * half
            qz = mx_ref.quantize(z.astype(BF))
            back = np.argsort(n, axis=1)
            p = [mx_ref.matmul(pick(lay[r], np.arange(128 * b, 128 * b + 128)), qz) * np.float32(0.03125) for b in range(4)]
            made.append(tile([(t[r][:, b::4] + gpick(p[b], back)) * half for b in range(4)]))
            new.append(n)
        now, own = made, new
    y, ln = np.zeros((N, 128, C), np.float32), np.zeros((N, 8, C), np.float32)
    oc, osc = np.zeros((N, 128, 4 * C), np.uint8), np.zeros((N, 16, C), np.uint8)
    for r in range(N):
        q = mx_ref.quantize(now[r])
        y[r] = mx_ref.matmul(mx_ref.quantize(v[r]), q)
        ln[r] = own[r]
        oc[r], osc[r] = emit(q)
    return {"y": y, "ln": ln, "oc": oc, "osc": osc}

@@ -1,0 +1,384 @@
+from concourse.mybir import dt, AluOpType, ActivationFunctionType
+
+C = 256
+ROUNDS = (1, 2, 4)
+COPY = ActivationFunctionType.Copy
+IDENTITY = ActivationFunctionType.Identity
+LIFT = 65536.0
+CODES = "float8_e4m3fn_x4"
+
+SCRATCH = {
+    "flb": ("sbuf", [128, 16], "int32"),
+    "ft": ("sbuf", [128, 16], "uint16"), "f4": ("sbuf", [128, 64], "uint16"), "fr": ("sbuf", [128, C], "bfloat16"),
+    "ut": ("sbuf", [128, 512], "bfloat16"), "uq": ("sbuf", [128, 128], CODES), "up": ("sbuf", [128, 128], "uint8"),
+    "urq": ("sbuf", [128, 128], CODES), "urp": ("sbuf", [128, 128], "uint8"),
+    "vt": ("sbuf", [128, 512], "bfloat16"), "vq": ("sbuf", [128, 128], CODES), "vp": ("sbuf", [128, 128], "uint8"),
+    "wq": ("sbuf", [128, 512], CODES), "wp": ("sbuf", [128, 512], "uint8"),
+    "ew": ("sbuf", [128, 516], "bfloat16"), "eq": ("sbuf", [128, 512], CODES), "ep": ("sbuf", [128, 512], "uint8"),
+    "xf": ("sbuf", [128, 1024], "bfloat16"), "qf": ("sbuf", [128, C], CODES), "pf": ("sbuf", [128, C], "uint8"),
+    "zt": ("sbuf", [128, 1024], "bfloat16"), "qz": ("sbuf", [128, C], CODES), "pz": ("sbuf", [128, C], "uint8"),
+    "fh": ("sbuf", [128, 1024], "bfloat16"), "zf": ("sbuf", [128, 1024], "bfloat16"), "pb": ("sbuf", [128, 1024], "float32"),
+    "wi": ("sbuf", [128, 512], "bfloat16"), "ie": ("sbuf", [128, 516], "float32"), "ia": ("sbuf", [128, 516], "float32"),
+    "wcol": ("sbuf", [128, 1], "float32"), "jm": ("sbuf", [128, C], "int32"), "jm2": ("sbuf", [128, C], "int32"),
+    "thr": ("sbuf", [128, C], "float32"), "rst": ("sbuf", [128, C], "bfloat16"), "cu": ("sbuf", [128, C], "bfloat16"),
+    "k1": ("sbuf", [128, C], "float32"), "sc0": ("sbuf", [128, 1], "float32"), "scc": ("sbuf", [128, 1], "float32"),
+    "pq": ("sbuf", [128, 16], "int32"), "pq2": ("sbuf", [128, 16], "int32"), "cj": ("sbuf", [128, 16], "float32"),
+    "jj": ("sbuf", [128, 16], "float32"), "jh": ("sbuf", [128, 16], "float32"), "oi": ("sbuf", [128, 8], "int32"), "ou": ("sbuf", [128, 8], "uint16"),
+    "mb": ("sbuf", [128, C], "bfloat16"), "ms": ("sbuf", [128, C], "bfloat16"), "scn": ("sbuf", [128, C], "bfloat16"), "scr": ("sbuf", [128, C], "bfloat16"),
+    "eh": ("sbuf", [128, 16], "float32"), "ed": ("sbuf", [128, 16], "float32"),
+    "pk": ("sbuf", [128, 48], "float32"), "ts": ("sbuf", [128, 48], "float32"), "t0": ("sbuf", [128, 32], "uint16"),
+    "tt": ("sbuf", [128, 48], "uint16"), "wa": ("sbuf", [128, 512], "bfloat16"), "wb": ("sbuf", [128, 512], "bfloat16"),
+    "ar": ("sbuf", [128, C], "bfloat16"), "at": ("sbuf", [128, 16], "uint16"),
+    "ir": ("sbuf", [128, C], "bfloat16"), "iv": ("sbuf", [128, C], "bfloat16"),
+    "lnf": ("sbuf", [128, C], "float32"), "yb": ("sbuf", [128, C], "float32"),
+    "psa": ("psum", [128, 2048], "float32"), "psb": ("psum", [128, 2048], "float32"),
+    "el0": ("sbuf", [128, 16], "int32"), "el1": ("sbuf", [128, 16], "uint16"), "el2": ("sbuf", [128, 16], "uint16"),
+}
+for _k in range(4):
+    SCRATCH["xt%d" % _k] = ("sbuf", [128, 1024], "bfloat16")
+    SCRATCH["qx%d" % _k] = ("sbuf", [128, C], CODES)
+    SCRATCH["px%d" % _k] = ("sbuf", [128, C], "uint8")
+for _k in range(3):
+    SCRATCH["lq%d" % _k] = ("sbuf", [128, C], CODES)
+    SCRATCH["lp%d" % _k] = ("sbuf", [128, C], "uint8")
+    SCRATCH["st%d" % _k] = ("sbuf", [128, 48], "bfloat16")
+    SCRATCH["sl%d" % _k] = ("sbuf", [128, 48], "bfloat16")
+    SCRATCH["rr%d" % _k] = ("sbuf", [128, C], "bfloat16")
+    SCRATCH["rt%d" % _k] = ("sbuf", [128, 16], "uint16")
+    SCRATCH["it%d" % _k] = ("sbuf", [128, 16], "uint16")
+SEMAPHORES = (["cv", "cs", "cp", "cg", "lo", "lf", "lx", "lu", "lv", "lw", "lws", "out"]
+              + ["%s%d" % (a, k) for a in ("ar_s", "ar_l", "ar_d") for k in range(3)])
+
+
+def rank_program(g, core, T, topo):
+    rank = T.rank_of(core)
+    if rank is None:
+        return
+    V, S, P = g.vector, g.scalar, g.tensor
+    queues = {"v": V, "s": S, "p": P, "g": g, "y": g.sync}
+    own = {"v": "cv", "s": "cs", "p": "cp", "g": "cg"}
+    known = {q: {} for q in queues}
+    snap = {}
+    total = {}
+    wrote, read = {}, {}
+
+    def covered(k, d):
+        return k.get(d[0], 0) >= d[1]
+
+    def wait(q, deps):
+        best = {}
+        for d in deps:
+            if not covered(known[q], d):
+                best[d[0]] = max(best.get(d[0], 0), d[1])
+        deps = list(best.items())
+        for d in deps:
+            if any(o != d and covered(snap[o], d) for o in deps):
+                continue
+            queues[q].wait_ge(T.sem[d[0]], d[1])
+        for d in deps:
+            known[q][d[0]] = max(known[q].get(d[0], 0), d[1])
+            for s, n in snap[d].items():
+                known[q][s] = max(known[q].get(s, 0), n)
+
+    def needs(reads, writes):
+        deps = [wrote[t] for t in reads]
+        for t in writes:
+            if t in wrote:
+                deps.append(wrote[t])
+            deps += read.get(t, [])
+        return deps
+
+    def op(q, call, reads, writes, sem=None, inc=1):
+        wait(q, needs(reads, writes))
+        name = sem or own[q]
+        ins = call()
+        ins.then_inc(T.sem[name], inc)
+        total[name] = total.get(name, 0) + inc
+        me = (name, total[name])
+        snap[me] = dict(known[q])
+        for t in reads:
+            read.setdefault(t, []).append(me)
+        for t in writes:
+            wrote[t], read[t] = me, []
+
+    def arrives(sem, n, tokens):
+        total[sem] = total.get(sem, 0) + n
+        for t in tokens:
+            wrote[t] = (sem, total[sem])
+        snap[(sem, total[sem])] = {}
+
+    def send(dst, out, in_, sem, reads):
+        wait("g", needs(reads, []))
+        rid, pid, _ = topo.addr(dst)
+        g.remote_dma(out, in_, T.sem[sem], T.sem.lo, pid, rid, topo.mask(core, dst))
+        total["lo"] = total.get("lo", 0) + len(topo.engines(core, dst))
+
+    def tcopy(out, in_, r, w):
+        op("v", lambda: V.tensor_copy(out, in_), r, w)
+
+    def tts(out, in0, s1, s2, o0, o1, r, w):
+        if o1 is None:
+            op("v", lambda: V.tensor_scalar(out, in0, s1, None, o0), r, w)
+        else:
+            op("v", lambda: V.tensor_scalar(out, in0, s1, s2, o0, o1), r, w)
+
+    def ttt(out, a, b, o, r, w):
+        op("v", lambda: V.tensor_tensor(out, a, b, o), r, w)
+
+    def fill(ap, value, w):
+        op("v", lambda: V.memset(ap, value), [], w)
+
+    def quant(q, p, t, r, w):
+        op("v", lambda: V.quantize_mx(q, p, t), r, w)
+
+    def act(out, in_, r, w, scale=None):
+        if scale is None:
+            op("s", lambda: S.activation(out, in_, COPY), r, w)
+        else:
+            op("s", lambda: S.activation(out, in_, COPY, scale=scale), r, w)
+
+    def mm(out, a, ap, b, bp, start, stop, r, w):
+        op("p", lambda: P.matmul_mx(out, a, ap, b, bp, start, stop), r, w)
+
+    def iota(out, pattern, base, cm, w, small=False):
+        if small:
+            op("g", lambda: g.iota(out, pattern, base, cm, allow_small_or_imprecise_dtypes=True), [], w)
+        else:
+            op("g", lambda: g.iota(out, pattern, base, cm), [], w)
+
+    A = AluOpType
+
+    def scan(row, r, w="scn"):
+        op("v", lambda: V.tensor_tensor_scan(T[w][:, 0:C], T.cu[:, 0:C], row[:, 0:C], 0.0, A.mult, A.add), r + ["cu"], [w])
+
+    def table(out, bias, w, s="scn"):
+        tts(out, T[s][:, 15:C:16], T.scc[:, 0:1], bias, A.mult, A.add, [s, "scc"], w)
+
+    spare = []
+
+    def hop(out, w, window, reads, off, oname, c0, n=8):
+        act(out[:, 0:16 * n], window.indirect(off[:, c0:c0 + n]), reads + [oname], [w + ".s"])
+        tcopy(out[:, 16 * n:C], window.indirect(off[:, c0 + n:c0 + 16]), reads + [oname], [w + ".v"])
+        if spare:
+            spare.pop(0)()
+
+    op("s", lambda: S.dma_start(T.flb[:], T.fl[:]), [], ["flb"], "lf", 16)
+    op("y", lambda: g.sync.dma_start(T.xt0[:], T.x[:]), [], ["xt0.%d" % b for b in range(4)], "lx", 16)
+    op("s", lambda: S.dma_start(T.ut[:], T.u[:]), [], ["ut"], "lu", 16)
+    wait("y", [wrote["xt0.0"]])
+    op("y", lambda: g.sync.dma_start(T.wq[:, 0:512].bitcast(dt.uint8), T.wc[:]), [], ["wq"], "lw", 16)
+    op("y", lambda: g.sync.dma_start(T.wp[:, 0:512], T.ws[:]), [], ["wp"], "lws", 16)
+    op("y", lambda: g.sync.dma_start(T.vt[:], T.v[:]), [], ["vt"], "lv", 16)
+    iota(T.jm[:], [[1, C]], 0, -1, ["jm"])
+    iota(T.oi[:], [[16, 8]], 0, 0, ["oi"])
+    iota(T.pq[:], [[0, 16]], 0, 1, ["pq"])
+    iota(T.cj[:], [[16, 16]], 256, 0, ["cj"], True)
+    iota(T.wcol[:], [[0, 1]], -252, 4, ["wcol"], True)
+    iota(T.ie[:], [[1, 516]], -4, -4, ["ie"], True)
+    first = T.cores[rank ^ ROUNDS[0]]
+    send(first, T.el0[:], T.flb[:], "ar_l0", ["flb"])
+    arrives("ar_l0", len(topo.engines(first, core)), ["el0"])
+    tts(T.jm2[:], T.jm[:], 15, None, A.bitwise_and, None, ["jm"], ["jm2"])
+    tcopy(T.ou[:], T.oi[:], ["oi"], ["ou"])
+    fill(T.st0[:], -1.0, ["st0"])
+    tts(T.thr[:], T.jm2[:], 0.0, 1.0e29, A.not_equal, A.mult, ["jm2"], ["thr"])
+    tts(T.rst[:], T.jm2[:], 0.0, None, A.not_equal, None, ["jm2"], ["rst"])
+    fill(T.st0[:, 0:48:3], 0.0, ["st0"])
+    tts(T.sc0[:], T.jm2[:, 15:16], 0.0, 1.0 - 1.0 / LIFT, A.is_equal, A.mult, ["jm2"], ["sc0"])
+    tts(T.pq2[:], T.pq[:], 15, None, A.bitwise_and, None, ["pq"], ["pq2"])
+    tts(T.scc[:], T.sc0[:], 1.0 / LIFT, None, A.add, None, ["sc0"], ["scc"])
+    ttt(T.jj[:], T.pq2[:], T.cj[:], A.add, ["pq2", "cj"], ["jj"])
+    tcopy(T.ft[:], T.flb[:], ["flb"], ["ft"])
+    tts(T.k1[:], T.jm2[:], 1.0, LIFT - 1.0, A.is_equal, A.mult, ["jm2"], ["k1"])
+    quant(T.uq[:, 0:128], T.up[:, 0:128], T.ut[:, 0:512], ["ut"], ["uq"])
+    tts(T.jh[:], T.jj[:], 0.5, None, A.mult, None, ["jj"], ["jh"])
+    op("v", lambda: V.tensor_copy(T.urq[:, 0:128].bitcast(dt.uint32), T.uq[:, 0:128].bitcast(dt.uint32).indirect(T.ou[:, 0:8])), ["uq", "ou"], ["urq"])
+    act(T.urp[:, 0:128], T.up[:, 0:128].indirect(T.ou[:, 0:8]), ["uq", "ou"], ["urp"])
+    op("s", lambda: S.activation(T.ia[:], T.ie[:], ActivationFunctionType.Abs), ["ie"], ["ia"])
+    op("s", lambda: S.activation(T.ew[:], T.ia[:], ActivationFunctionType.Relu, bias=1.0, scale=-1.0), ["ia"], ["ew"])
+    op("s", lambda: S.activation(T.wi[:], T.ie[:, 0:512], IDENTITY, bias=T.wcol[:, 0:1]), ["ie", "wcol"], ["wi"])
+    act(T.wa[:, C:2 * C], T.wi[:, C:2 * C], ["wi"], ["wa.k"])
+    act(T.wb[:, C:2 * C], T.wi[:, C:2 * C], ["wi"], ["wb.k"])
+
+    win = (T.wa, T.wb)
+    wn = ("wa", "wb")
+    for k, m in enumerate(ROUNDS):
+        d = T.cores[rank ^ m]
+        ne = len(topo.engines(d, core))
+        xt, qx, px = T["xt%d" % k], T["qx%d" % k], T["px%d" % k]
+        lq, lp, st, sl, el = T["lq%d" % k], T["lp%d" % k], T["st%d" % k], T["sl%d" % k], T["el%d" % k]
+        rr, rt, it = T["rr%d" % k], T["rt%d" % k], T["it%d" % k]
+        Xt = ["xt%d.%d" % (k, b) for b in range(4)]
+        Qx = ["qx%d.0" % k, "qx%d.1" % k]
+        for h in range(2):
+            c = 128 * h
+            quant(qx[:, c:c + 128], px[:, c:c + 128], xt[:, 4 * c:4 * c + 512], Xt, [Qx[h]])
+            mm(T.psb[:, 4 * c:4 * c + 128], T.urq[:, 0:128], T.urp[:, 0:128], qx[:, c:c + 128], px[:, c:c + 128], True, True, ["urq", "urp", Qx[h]], ["psb%d" % h])
+        for h in range(2):
+            c = 128 * h
+            ttt(T.mb[:, c:c + 128], T.psb[:, 4 * c:4 * c + 128], T.thr[:, c:c + 128], A.is_gt, ["psb%d" % h, "thr"], ["mb%d" % h])
+        for h in range(2):
+            op("v", lambda c=128 * h: V.tensor_tensor_scan(T.ms[:, c:c + 128], T.rst[:, c:c + 128], T.mb[:, c:c + 128], 0.0, A.mult, A.add),
+               ["rst", "mb%d" % h], ["ms%d" % h])
+        tts(st[:, 1:48:3], T.ms[:, 15:C:16], 2.0, -1.0, A.mult, A.add, ["ms0", "ms1"], ["st%d" % k])
+        send(d, sl[:], st[:], "ar_s%d" % k, ["st%d" % k])
+        arrives("ar_s%d" % k, ne, ["sl%d" % k])
+        send(d, lq[:, 0:C].bitcast(dt.uint8), qx[:, 0:C].bitcast(dt.uint8), "ar_d%d" % k, Qx)
+        send(d, lp[:, 0:C], px[:, 0:C], "ar_d%d" % k, Qx)
+        arrives("ar_d%d" % k, 2 * ne, ["lq%d" % k])
+        fsrc, fname = (T.ft, "ft") if k == 0 else (T["rt%d" % (k - 1)], "rt%d" % (k - 1))
+        frow, frname = (T.fr, "fr") if k == 0 else (T["rr%d" % (k - 1)], "rr%d" % (k - 1))
+        lay = ((1, 2, 3), (0,)) if k == 0 else ((2, 3), (0, 1))
+        for b in lay[0] + lay[1]:
+            tts(T.f4[:, 16 * b:16 * b + 16], fsrc[:], 4.0, float(b), A.mult, A.add, [fname], ["f4.%d" % b])
+        for b in lay[0]:
+            act(T.xf[:, b:1024:4], xt[:, 0:1024].indirect(T.f4[:, 16 * b:16 * b + 16]), Xt + ["f4.%d" % b], ["xf%d" % b])
+        for b in lay[1]:
+            tcopy(T.xf[:, b:1024:4], xt[:, 0:1024].indirect(T.f4[:, 16 * b:16 * b + 16]), Xt + ["f4.%d" % b], ["xf%d" % b])
+        if k == 0:
+            for b in range(4):
+                quant(T.eq[:, 128 * b:128 * b + 128], T.ep[:, 128 * b:128 * b + 128], T.ew[:, 4 - b:516 - b], ["ew"], ["eq%d" % b])
+        tts(T.eh[:], el[:], 0.5, None, A.mult, None, ["el%d" % k], ["eh"])
+        if k == 0:
+            ttt(T.cu[:], T.k1[:], T.rst[:], A.add, ["k1", "rst"], ["cu"])
+        ttt(T.ed[:], T.eh[:], T.jh[:], A.subtract, ["eh", "jh"], ["ed"])
+        ttt(T.pk[:, 1:48:3], T.eh[:], T.jh[:], A.add, ["eh", "jh"], ["pk1"])
+        ttt(T.pk[:, 0:48:3], T.ed[:], st[:, 1:48:3], A.mult, ["ed", "st%d" % k], ["pk0"])
+        tts(T.pk[:, 2:48:3], T.pk[:, 1:48:3], 2.0, None, A.mult, None, ["pk1"], ["pk2"])
+        for b in range(4):
+            mm(T.psa[:, 512 * b:512 * b + C], T.eq[:, 128 * b:128 * b + 128], T.ep[:, 128 * b:128 * b + 128], qx[:, 0:C], px[:, 0:C], True, True,
+               ["eq%d" % b] + Qx, ["psa%d" % b])
+
+        def quant_f(h):
+            c = 128 * h
+            quant(T.qf[:, c:c + 128], T.pf[:, c:c + 128], T.xf[:, 4 * c:4 * c + 512], ["xf%d" % b for b in range(4)], ["qf%d" % h])
+
+        def meet_products():
+            for b in range(4):
+                e, ep, o = T.eq[:, 128 * b:128 * b + 128], T.ep[:, 128 * b:128 * b + 128], T.psb[:, 512 * b:512 * b + C]
+                mm(o, e, ep, T.qf[:, 0:C], T.pf[:, 0:C], True, False, ["eq%d" % b, "qf0", "qf1"], ["psb%d" % b])
+                mm(o, e, ep, lq[:, 0:C], lp[:, 0:C], False, True, ["eq%d" % b, "lq%d" % k], ["psb%d" % b])
+
+        def half(b):
+            act(T.fh[:, C * b:C * b + C], T.psa[:, 512 * b:512 * b + C], ["psa%d" % b], ["fh%d" % b], 0.5)
+
+        def meet(b):
+            act(T.zf[:, C * b:C * b + C], T.psb[:, 512 * b:512 * b + C], ["psb%d" % b], ["zf%d" % b], 0.5)
+
+        if k > 0:
+            quant_f(0)
+            quant_f(1)
+            meet_products()
+            for b in range(4):
+                half(b)
+        op("v", lambda: V.tensor_tensor_scan(T.ts[:], sl[:], T.pk[:], 0.0, A.mult, A.add), ["sl%d" % k, "pk0", "pk1", "pk2"], ["ts"])
+        tcopy(T.t0[:, 0:16], T.ts[:, 1:48:3], ["ts"], ["t0"])
+        spare.append(lambda: tcopy(T.t0[:, 16:32], T.ts[:, 2:48:3], ["ts"], ["t0e"]))
+        if k == 0:
+            spare.append(lambda: quant_f(0))
+            spare.append(lambda: quant_f(1))
+            for n in ("st1", "st2"):
+                spare.append(lambda n=n: fill(T[n][:], -1.0, [n]))
+                spare.append(lambda n=n: fill(T[n][:, 0:48:3], 0.0, [n]))
+            spare.append(lambda: quant(T.vq[:, 0:128], T.vp[:, 0:128], T.vt[:, 0:512], ["vt"], ["vq"]))
+        hop(T.wa, "wa", T.wi[:, 0:512], ["wi"], T.t0, "t0", 0)
+        off, oname, c0, a = T.t0, "t0", 0, 0
+        for i in range(4):
+            for _ in range(3):
+                hop(win[1 - a], wn[1 - a], win[a][:, 0:512], [wn[a] + ".v", wn[a] + ".s", wn[a] + ".k"], off, oname, c0)
+                a = 1 - a
+            if i < 3:
+                if i == 0 and k == 0:
+                    meet_products()
+                    half(0)
+                    half(1)
+                if i == 1:
+                    meet(0)
+                    meet(1)
+                if i == 2:
+                    meet(2)
+                    if k == 0:
+                        meet(3)
+                scan(win[a], [wn[a] + ".v", wn[a] + ".s"])
+                table(T.tt[:, 16 * i:16 * i + 16], 256.25, ["tt%d" % i])
+                off, oname, c0 = T.tt, "tt%d" % i, 16 * i
+        hop(T.ar, "ar", win[a][:, 0:512], [wn[a] + ".v", wn[a] + ".s", wn[a] + ".k"], T.t0, "t0e", 16)
+        if k == 0:
+            act(T.fr[:], T.wi[:, C:2 * C].indirect(T.ft[:, 0:16]), ["wi", "ft"], ["fr"])
+        else:
+            meet(3)
+        scan(T.ar, ["ar.v", "ar.s"])
+        table(T.at[:], 0.25, ["at"])
+
+        def list_row():
+            act(rr[:], frow[:, 0:C].indirect(T.at[:, 0:16]), [frname, "at"], ["rr%d" % k])
+
+        def list_out():
+            table(rt[:], 0.25, ["rt%d" % k], "scr")
+            nd = T.cores[rank ^ ROUNDS[k + 1]]
+            send(nd, T["el%d" % (k + 1)][:], rt[:], "ar_l%d" % (k + 1), ["rt%d" % k])
+            arrives("ar_l%d" % (k + 1), len(topo.engines(nd, core)), ["el%d" % (k + 1)])
+
+        def quant_z():
+            for h in range(2):
+                c = 128 * h
+                quant(T.qz[:, c:c + 128], T.pz[:, c:c + 128], T.zt[:, 4 * c:4 * c + 512], ["zt%d" % b for b in range(4)], ["qz%d" % h])
+
+        if k == 0:
+            list_row()
+        for b in range(4):
+            f = tcopy if b == 0 else act
+            f(T.zt[:, b:1024:4], T.zf[:, C * b:C * b + C].indirect(T.at[:, 0:16]), ["zf%d" % b, "at"], ["zt%d" % b])
+        if k == 0:
+            scan(rr, ["rr%d" % k], "scr")
+            list_out()
+            tcopy(T.ir[:, 0:C].indirect(rt[:, 0:16]), T.wi[:, C:2 * C], ["wi", "rt%d" % k], ["ir"])
+            quant_z()
+            scan(T.ir, ["ir"])
+            table(it[:], 0.25, ["it%d" % k])
+        else:
+            tcopy(T.ir[:, 0:C].indirect(T.at[:, 0:16]), T.wi[:, C:2 * C], ["wi", "at"], ["ir"])
+            quant_z()
+            hop(T.iv, "iv", T.ir[:, 0:C], ["ir"], T["it%d" % (k - 1)], "it%d" % (k - 1), 0, 12)
+            list_row()
+            scan(T.iv, ["iv.v", "iv.s"])
+            table(it[:], 0.25, ["it%d" % k])
+            if k < 2:
+                scan(rr, ["rr%d" % k], "scr")
+        cuts = ((0, 0, 128, T.psb[:, 0:128], "psb0"), (0, 128, C, T.psa[:, 0:128], "psa0")) + tuple(
+            (b, 0, C, T.psb[:, 512 * b:512 * b + C], "psb%d" % b) for b in (1, 2, 3))
+        for b, lo, hi, o, n in cuts:
+            mm(o, T.wq[:, 128 * b:128 * b + 128], T.wp[:, 128 * b:128 * b + 128], T.qz[:, lo:hi], T.pz[:, lo:hi], True, True,
+               ["wq", "wp"] + ["qz%d" % h for h in range(2) if lo <= 128 * h < hi], [n])
+        for b, lo, hi, o, n in cuts:
+            if k == 0 and b > 1:
+                half(b)
+            act(T.pb[:, C * b + lo:C * b + hi], o, [n], ["pb%d.%d" % (b, lo)], 0.015625)
+        xn = T["xt%d" % (k + 1)]
+        for b in range(4):
+            ttt(xn[:, b:1024:4], T.pb[:, C * b:C * b + C].indirect(it[:, 0:16]), T.fh[:, C * b:C * b + C], A.add,
+                ["pb%d.%d" % (c, lo) for c, lo, hi, o, n in cuts if c == b] + ["it%d" % k, "fh%d" % b], ["xt%d.%d" % (k + 1, b)])
+            if b == 0 and k == 1:
+                list_out()
+    act(T.lnf[:], T.rr2[:], ["rr2"], ["lnf"])
+    op("y", lambda: g.sync.dma_start(T.ln[:], T.lnf[0:128:16, :]), ["lnf"], ["ln"], "out", 16)
+    Q3 = ["qx3.0", "qx3.1"]
+    for h in range(2):
+        c = 128 * h
+        quant(T.qx3[:, c:c + 128], T.px3[:, c:c + 128], T.xt3[:, 4 * c:4 * c + 512], ["xt3.%d" % b for b in range(4)], [Q3[h]])
+        mm(T.psa[:, 4 * c:4 * c + 128], T.vq[:, 0:128], T.vp[:, 0:128], T.qx3[:, c:c + 128], T.px3[:, c:c + 128], True, True, ["vq", Q3[h]], ["psa%d" % h])
+    op("y", lambda: g.sync.dma_start(T.oc[:, 0:4 * C], T.qx3[:, 0:C].bitcast(dt.uint8)), Q3, ["oc"], "out", 16)
+
+    def scales(q, queue, i):
+        op(q, lambda: queue.dma_start(T.osc[4 * i:4 * i + 4, 0:C], T.px3[32 * i:32 * i + 4, 0:C]), Q3, ["osc%d" % i], "out", 16)
+
+    scales("y", g.sync, 0)
+    scales("y", g.sync, 1)
+    tcopy(T.yb[:, 0:128], T.psa[:, 0:128], ["psa0"], ["y0"])
+    act(T.yb[:, 128:C], T.psa[:, 512:640], ["psa1"], ["y1"])
+    op("y", lambda: g.sync.dma_start(T.y[:, 0:128], T.yb[:, 0:128]), ["y0"], ["yo0"], "out", 16)
+    op("s", lambda: S.dma_start(T.y[:, 128:C], T.yb[:, 128:C]), ["y1"], ["yo1"], "out", 16)
+    scales("s", S, 2)
+    scales("s", S, 3)
+    for s, n in sorted(total.items()):
+        g.wait_ge(T.sem[s], n)

@@ -3,9 +3,10 @@ from concourse.mybir import dt, AluOpType, ActivationFunctionType
 C = 256
 ROUNDS = (1, 2, 4)
 COPY = ActivationFunctionType.Copy
-IDENTITY = ActivationFunctionType.Identity
 LIFT = 65536.0
 CODES = "float8_e4m3fn_x4"
+JUMPS = ((None, 2, 1, 1), (2, 3, 2, 1), (3, 5, 3, 2), (5, 8, 5, 3), (8, 13, 8, 5), (13, 21, 13, 8), (21, 34, 21, 13), (34, 55, 34, 21),
+         (None, 89, 55, 34), (89, "A", 89, "e"), ("A", 178, 89, 89), (None, "a", 178, "A"))
 
 SCRATCH = {
     "flb": ("sbuf", [128, 16], "int32"),
@@ -14,21 +15,24 @@ SCRATCH = {
     "urq": ("sbuf", [128, 128], CODES), "urp": ("sbuf", [128, 128], "uint8"),
     "vt": ("sbuf", [128, 512], "bfloat16"), "vq": ("sbuf", [128, 128], CODES), "vp": ("sbuf", [128, 128], "uint8"),
     "wq": ("sbuf", [128, 512], CODES), "wp": ("sbuf", [128, 512], "uint8"),
+    "one": ("sbuf", [128, 516], "bfloat16"),
     "ew": ("sbuf", [128, 516], "bfloat16"), "eq": ("sbuf", [128, 512], CODES), "ep": ("sbuf", [128, 512], "uint8"),
     "xf": ("sbuf", [128, 1024], "bfloat16"), "qf": ("sbuf", [128, C], CODES), "pf": ("sbuf", [128, C], "uint8"),
     "zt": ("sbuf", [128, 1024], "bfloat16"), "qz": ("sbuf", [128, C], CODES), "pz": ("sbuf", [128, C], "uint8"),
     "fh": ("sbuf", [128, 1024], "bfloat16"), "zf": ("sbuf", [128, 1024], "bfloat16"), "pb": ("sbuf", [128, 1024], "float32"),
-    "wi": ("sbuf", [128, 512], "bfloat16"), "ie": ("sbuf", [128, 516], "float32"), "ia": ("sbuf", [128, 516], "float32"),
-    "wcol": ("sbuf", [128, 1], "float32"), "jm": ("sbuf", [128, C], "int32"), "jm2": ("sbuf", [128, C], "int32"),
+    "wi": ("sbuf", [128, 512], "bfloat16"),
+    "jm": ("sbuf", [128, C], "int32"), "jm2": ("sbuf", [128, C], "int32"),
     "thr": ("sbuf", [128, C], "float32"), "rst": ("sbuf", [128, C], "bfloat16"), "cu": ("sbuf", [128, C], "bfloat16"),
     "k1": ("sbuf", [128, C], "float32"), "sc0": ("sbuf", [128, 1], "float32"), "scc": ("sbuf", [128, 1], "float32"),
     "pq": ("sbuf", [128, 16], "int32"), "pq2": ("sbuf", [128, 16], "int32"), "cj": ("sbuf", [128, 16], "float32"),
     "jj": ("sbuf", [128, 16], "float32"), "jh": ("sbuf", [128, 16], "float32"), "oi": ("sbuf", [128, 8], "int32"), "ou": ("sbuf", [128, 8], "uint16"),
-    "mb": ("sbuf", [128, C], "bfloat16"), "ms": ("sbuf", [128, C], "bfloat16"), "scn": ("sbuf", [128, C], "bfloat16"), "scr": ("sbuf", [128, C], "bfloat16"),
+    "mb": ("sbuf", [128, C], "bfloat16"), "ms": ("sbuf", [128, C], "bfloat16"),
+    "sc1": ("sbuf", [128, C], "bfloat16"), "sc2": ("sbuf", [128, C], "bfloat16"), "scr": ("sbuf", [128, C], "bfloat16"),
     "eh": ("sbuf", [128, 16], "float32"), "ed": ("sbuf", [128, 16], "float32"),
-    "pk": ("sbuf", [128, 48], "float32"), "ts": ("sbuf", [128, 48], "float32"), "t0": ("sbuf", [128, 32], "uint16"),
-    "tt": ("sbuf", [128, 48], "uint16"), "wa": ("sbuf", [128, 512], "bfloat16"), "wb": ("sbuf", [128, 512], "bfloat16"),
-    "ar": ("sbuf", [128, C], "bfloat16"), "at": ("sbuf", [128, 16], "uint16"),
+    "pk": ("sbuf", [128, 48], "float32"), "ts": ("sbuf", [128, 48], "float32"),
+    "tt": ("sbuf", [128, 16 * 12], "uint16"),
+    "w0": ("sbuf", [128, 512], "bfloat16"), "w1": ("sbuf", [128, 512], "bfloat16"), "w2": ("sbuf", [128, 512], "bfloat16"),
+    "aa": ("sbuf", [128, C], "bfloat16"), "ar": ("sbuf", [128, C], "bfloat16"), "at": ("sbuf", [128, 16], "uint16"),
     "ir": ("sbuf", [128, C], "bfloat16"), "iv": ("sbuf", [128, C], "bfloat16"),
     "lnf": ("sbuf", [128, C], "float32"), "yb": ("sbuf", [128, C], "float32"),
     "psa": ("psum", [128, 2048], "float32"), "psb": ("psum", [128, 2048], "float32"),
@@ -148,176 +152,188 @@ def rank_program(g, core, T, topo):
 
     A = AluOpType
 
-    def scan(row, r, w="scn"):
+    def scan(row, r, w):
         op("v", lambda: V.tensor_tensor_scan(T[w][:, 0:C], T.cu[:, 0:C], row[:, 0:C], 0.0, A.mult, A.add), r + ["cu"], [w])
 
-    def table(out, bias, w, s="scn"):
+    def table(out, bias, w, s):
         tts(out, T[s][:, 15:C:16], T.scc[:, 0:1], bias, A.mult, A.add, [s, "scc"], w)
 
-    spare = []
-
-    def hop(out, w, window, reads, off, oname, c0, n=8):
+    def hop_s(out, w, window, reads, off, oname, c0, n):
         act(out[:, 0:16 * n], window.indirect(off[:, c0:c0 + n]), reads + [oname], [w + ".s"])
+
+    def hop_v(out, w, window, reads, off, oname, c0, n):
         tcopy(out[:, 16 * n:C], window.indirect(off[:, c0 + n:c0 + 16]), reads + [oname], [w + ".v"])
-        if spare:
-            spare.pop(0)()
+
+    def hop(*a):
+        hop_s(*a)
+        hop_v(*a)
 
     op("s", lambda: S.dma_start(T.flb[:], T.fl[:]), [], ["flb"], "lf", 16)
-    op("y", lambda: g.sync.dma_start(T.xt0[:], T.x[:]), [], ["xt0.%d" % b for b in range(4)], "lx", 16)
-    op("s", lambda: S.dma_start(T.ut[:], T.u[:]), [], ["ut"], "lu", 16)
-    wait("y", [wrote["xt0.0"]])
-    op("y", lambda: g.sync.dma_start(T.wq[:, 0:512].bitcast(dt.uint8), T.wc[:]), [], ["wq"], "lw", 16)
-    op("y", lambda: g.sync.dma_start(T.wp[:, 0:512], T.ws[:]), [], ["wp"], "lws", 16)
-    op("y", lambda: g.sync.dma_start(T.vt[:], T.v[:]), [], ["vt"], "lv", 16)
+    op("y", lambda: g.sync.dma_start(T.ut[:], T.u[:]), [], ["ut"], "lu", 16)
+    op("y", lambda: g.sync.dma_start(T.xt0[:], T.x[:]), [], ["xt0.%d.%d" % (b, h) for b in range(4) for h in range(2)], "lx", 16)
     iota(T.jm[:], [[1, C]], 0, -1, ["jm"])
     iota(T.oi[:], [[16, 8]], 0, 0, ["oi"])
+    iota(T.wi[:], [[1, 512]], -C, 0, ["wi"], True)
     iota(T.pq[:], [[0, 16]], 0, 1, ["pq"])
-    iota(T.cj[:], [[16, 16]], 256, 0, ["cj"], True)
-    iota(T.wcol[:], [[0, 1]], -252, 4, ["wcol"], True)
-    iota(T.ie[:], [[1, 516]], -4, -4, ["ie"], True)
+    iota(T.cj[:], [[16, 16]], C, 0, ["cj"], True)
     first = T.cores[rank ^ ROUNDS[0]]
     send(first, T.el0[:], T.flb[:], "ar_l0", ["flb"])
     arrives("ar_l0", len(topo.engines(first, core)), ["el0"])
+    fill(T.one[:], 1.0, ["one"])
+    fill(T.st0[:], -1.0, ["st0"])
+    op("g", lambda: g.affine_select(T.ew[:], T.one[:], [[1, 516]], A.is_equal, 0.0, -4, -4), ["one"], ["ew"])
+    fill(T.st0[:, 0:48:3], 0.0, ["st0"])
     tts(T.jm2[:], T.jm[:], 15, None, A.bitwise_and, None, ["jm"], ["jm2"])
     tcopy(T.ou[:], T.oi[:], ["oi"], ["ou"])
-    fill(T.st0[:], -1.0, ["st0"])
-    tts(T.thr[:], T.jm2[:], 0.0, 1.0e29, A.not_equal, A.mult, ["jm2"], ["thr"])
     tts(T.rst[:], T.jm2[:], 0.0, None, A.not_equal, None, ["jm2"], ["rst"])
-    fill(T.st0[:, 0:48:3], 0.0, ["st0"])
-    tts(T.sc0[:], T.jm2[:, 15:16], 0.0, 1.0 - 1.0 / LIFT, A.is_equal, A.mult, ["jm2"], ["sc0"])
-    tts(T.pq2[:], T.pq[:], 15, None, A.bitwise_and, None, ["pq"], ["pq2"])
-    tts(T.scc[:], T.sc0[:], 1.0 / LIFT, None, A.add, None, ["sc0"], ["scc"])
-    ttt(T.jj[:], T.pq2[:], T.cj[:], A.add, ["pq2", "cj"], ["jj"])
-    tcopy(T.ft[:], T.flb[:], ["flb"], ["ft"])
     tts(T.k1[:], T.jm2[:], 1.0, LIFT - 1.0, A.is_equal, A.mult, ["jm2"], ["k1"])
+    act(T.thr[:], T.rst[:], ["rst"], ["thr"], 1.0e29)
+    tts(T.sc0[:], T.jm2[:, 15:16], 0.0, 1.0 - 1.0 / LIFT, A.is_equal, A.mult, ["jm2"], ["sc0"])
+    ttt(T.cu[:], T.k1[:], T.rst[:], A.add, ["k1", "rst"], ["cu"])
+    tts(T.scc[:], T.sc0[:], 1.0 / LIFT, None, A.add, None, ["sc0"], ["scc"])
+    tcopy(T.ft[:], T.flb[:], ["flb"], ["ft"])
+    tts(T.pq2[:], T.pq[:], 15, None, A.bitwise_and, None, ["pq"], ["pq2"])
+    for n in ("w0", "w1", "w2"):
+        act(T[n][:, C:2 * C], T.wi[:, C:2 * C], ["wi"], [n + ".k"])
     quant(T.uq[:, 0:128], T.up[:, 0:128], T.ut[:, 0:512], ["ut"], ["uq"])
-    tts(T.jh[:], T.jj[:], 0.5, None, A.mult, None, ["jj"], ["jh"])
+    ttt(T.jj[:], T.pq2[:], T.cj[:], A.add, ["pq2", "cj"], ["jj"])
     op("v", lambda: V.tensor_copy(T.urq[:, 0:128].bitcast(dt.uint32), T.uq[:, 0:128].bitcast(dt.uint32).indirect(T.ou[:, 0:8])), ["uq", "ou"], ["urq"])
     act(T.urp[:, 0:128], T.up[:, 0:128].indirect(T.ou[:, 0:8]), ["uq", "ou"], ["urp"])
-    op("s", lambda: S.activation(T.ia[:], T.ie[:], ActivationFunctionType.Abs), ["ie"], ["ia"])
-    op("s", lambda: S.activation(T.ew[:], T.ia[:], ActivationFunctionType.Relu, bias=1.0, scale=-1.0), ["ia"], ["ew"])
-    op("s", lambda: S.activation(T.wi[:], T.ie[:, 0:512], IDENTITY, bias=T.wcol[:, 0:1]), ["ie", "wcol"], ["wi"])
-    act(T.wa[:, C:2 * C], T.wi[:, C:2 * C], ["wi"], ["wa.k"])
-    act(T.wb[:, C:2 * C], T.wi[:, C:2 * C], ["wi"], ["wb.k"])
+    act(T.fr[:], T.wi[:, C:2 * C].indirect(T.ft[:, 0:16]), ["wi", "ft"], ["fr"])
 
-    win = (T.wa, T.wb)
-    wn = ("wa", "wb")
+    def four(src, name, b):
+        tts(T.f4[:, 16 * b:16 * b + 16], src[:], 4.0, float(b), A.mult, A.add, [name], ["f4.%d" % b])
+
+    for b in range(4):
+        four(T.ft, "ft", b)
+
     for k, m in enumerate(ROUNDS):
         d = T.cores[rank ^ m]
         ne = len(topo.engines(d, core))
         xt, qx, px = T["xt%d" % k], T["qx%d" % k], T["px%d" % k]
         lq, lp, st, sl, el = T["lq%d" % k], T["lp%d" % k], T["st%d" % k], T["sl%d" % k], T["el%d" % k]
         rr, rt, it = T["rr%d" % k], T["rt%d" % k], T["it%d" % k]
-        Xt = ["xt%d.%d" % (k, b) for b in range(4)]
+        Xt = ["xt%d.%d.%d" % (k, b, h) for b in range(4) for h in range(2)]
         Qx = ["qx%d.0" % k, "qx%d.1" % k]
+        frow, frname = (T.fr, "fr") if k == 0 else (T["rr%d" % (k - 1)], "rr%d" % (k - 1))
+
+        def list_out(k):
+            table(T["rt%d" % k][:], 0.25, ["rt%d" % k], "scr")
+            nd = T.cores[rank ^ ROUNDS[k + 1]]
+            send(nd, T["el%d" % (k + 1)][:], T["rt%d" % k][:], "ar_l%d" % (k + 1), ["rt%d" % k])
+            arrives("ar_l%d" % (k + 1), len(topo.engines(nd, core)), ["el%d" % (k + 1)])
+
+        def lay(f, b):
+            f(T.xf[:, b:1024:4], xt[:, 0:1024].indirect(T.f4[:, 16 * b:16 * b + 16]), Xt + ["f4.%d" % b], ["xf%d" % b])
+
+        gaps = []
+        if k == 2:
+            gaps = [lambda: scan(frow, [frname], "scr"), lambda: list_out(k - 1)]
+        if k > 0:
+            gaps += [lambda b=b: four(T["rt%d" % (k - 1)], "rt%d" % (k - 1), b) for b in (2, 3, 0, 1)]
+
+        def gap(n=1):
+            for _ in range(n):
+                if gaps:
+                    gaps.pop(0)()
+
         for h in range(2):
             c = 128 * h
-            quant(qx[:, c:c + 128], px[:, c:c + 128], xt[:, 4 * c:4 * c + 512], Xt, [Qx[h]])
+            quant(qx[:, c:c + 128], px[:, c:c + 128], xt[:, 4 * c:4 * c + 512], Xt[h::2], [Qx[h]])
             mm(T.psb[:, 4 * c:4 * c + 128], T.urq[:, 0:128], T.urp[:, 0:128], qx[:, c:c + 128], px[:, c:c + 128], True, True, ["urq", "urp", Qx[h]], ["psb%d" % h])
+        gap()
+        if k == 0:
+            for b in (1, 2, 3):
+                lay(act, b)
         for h in range(2):
             c = 128 * h
             ttt(T.mb[:, c:c + 128], T.psb[:, 4 * c:4 * c + 128], T.thr[:, c:c + 128], A.is_gt, ["psb%d" % h, "thr"], ["mb%d" % h])
+            gap(1 - h)
         for h in range(2):
             op("v", lambda c=128 * h: V.tensor_tensor_scan(T.ms[:, c:c + 128], T.rst[:, c:c + 128], T.mb[:, c:c + 128], 0.0, A.mult, A.add),
                ["rst", "mb%d" % h], ["ms%d" % h])
+            gap(1 + h)
         tts(st[:, 1:48:3], T.ms[:, 15:C:16], 2.0, -1.0, A.mult, A.add, ["ms0", "ms1"], ["st%d" % k])
         send(d, sl[:], st[:], "ar_s%d" % k, ["st%d" % k])
         arrives("ar_s%d" % k, ne, ["sl%d" % k])
         send(d, lq[:, 0:C].bitcast(dt.uint8), qx[:, 0:C].bitcast(dt.uint8), "ar_d%d" % k, Qx)
         send(d, lp[:, 0:C], px[:, 0:C], "ar_d%d" % k, Qx)
         arrives("ar_d%d" % k, 2 * ne, ["lq%d" % k])
-        fsrc, fname = (T.ft, "ft") if k == 0 else (T["rt%d" % (k - 1)], "rt%d" % (k - 1))
-        frow, frname = (T.fr, "fr") if k == 0 else (T["rr%d" % (k - 1)], "rr%d" % (k - 1))
-        lay = ((1, 2, 3), (0,)) if k == 0 else ((2, 3), (0, 1))
-        for b in lay[0] + lay[1]:
-            tts(T.f4[:, 16 * b:16 * b + 16], fsrc[:], 4.0, float(b), A.mult, A.add, [fname], ["f4.%d" % b])
-        for b in lay[0]:
-            act(T.xf[:, b:1024:4], xt[:, 0:1024].indirect(T.f4[:, 16 * b:16 * b + 16]), Xt + ["f4.%d" % b], ["xf%d" % b])
-        for b in lay[1]:
-            tcopy(T.xf[:, b:1024:4], xt[:, 0:1024].indirect(T.f4[:, 16 * b:16 * b + 16]), Xt + ["f4.%d" % b], ["xf%d" % b])
+        gap(4)
         if k == 0:
+            wait("y", [wrote["sl0"]])
+            op("y", lambda: g.sync.dma_start(T.wq[:, 0:512].bitcast(dt.uint8), T.wc[:]), [], ["wq"], "lw", 16)
+            op("y", lambda: g.sync.dma_start(T.wp[:, 0:512], T.ws[:]), [], ["wp"], "lws", 16)
+            op("y", lambda: g.sync.dma_start(T.vt[:], T.v[:]), [], ["vt"], "lv", 16)
             for b in range(4):
                 quant(T.eq[:, 128 * b:128 * b + 128], T.ep[:, 128 * b:128 * b + 128], T.ew[:, 4 - b:516 - b], ["ew"], ["eq%d" % b])
-        tts(T.eh[:], el[:], 0.5, None, A.mult, None, ["el%d" % k], ["eh"])
-        if k == 0:
-            ttt(T.cu[:], T.k1[:], T.rst[:], A.add, ["k1", "rst"], ["cu"])
-        ttt(T.ed[:], T.eh[:], T.jh[:], A.subtract, ["eh", "jh"], ["ed"])
-        ttt(T.pk[:, 1:48:3], T.eh[:], T.jh[:], A.add, ["eh", "jh"], ["pk1"])
-        ttt(T.pk[:, 0:48:3], T.ed[:], st[:, 1:48:3], A.mult, ["ed", "st%d" % k], ["pk0"])
-        tts(T.pk[:, 2:48:3], T.pk[:, 1:48:3], 2.0, None, A.mult, None, ["pk1"], ["pk2"])
+            tts(T.jh[:], T.jj[:], 0.5, None, A.mult, None, ["jj"], ["jh"])
+            lay(tcopy, 0)
+        else:
+            for b in (2, 3):
+                lay(act, b)
+            for b in (0, 1):
+                lay(tcopy, b)
         for b in range(4):
             mm(T.psa[:, 512 * b:512 * b + C], T.eq[:, 128 * b:128 * b + 128], T.ep[:, 128 * b:128 * b + 128], qx[:, 0:C], px[:, 0:C], True, True,
                ["eq%d" % b] + Qx, ["psa%d" % b])
+        for b in range(4):
+            act(T.fh[:, C * b:C * b + C], T.psa[:, 512 * b:512 * b + C], ["psa%d" % b], ["fh%d" % b], 0.5)
 
         def quant_f(h):
             c = 128 * h
             quant(T.qf[:, c:c + 128], T.pf[:, c:c + 128], T.xf[:, 4 * c:4 * c + 512], ["xf%d" % b for b in range(4)], ["qf%d" % h])
 
-        def meet_products():
+        tts(T.eh[:], el[:], 0.5, None, A.mult, None, ["el%d" % k], ["eh"])
+        quant_f(0)
+        ttt(T.ed[:], T.eh[:], T.jh[:], A.subtract, ["eh", "jh"], ["ed"])
+        ttt(T.pk[:, 1:48:3], T.eh[:], T.jh[:], A.add, ["eh", "jh"], ["pk1"])
+        quant_f(1)
+        ttt(T.pk[:, 0:48:3], T.ed[:], st[:, 1:48:3], A.mult, ["ed", "st%d" % k], ["pk0"])
+        tts(T.pk[:, 2:48:3], T.pk[:, 1:48:3], 2.0, None, A.mult, None, ["pk1"], ["pk2"])
+        for q, p, r, start in ((T.qf, T.pf, ["qf0", "qf1"], True), (lq, lp, ["lq%d" % k], False)):
             for b in range(4):
-                e, ep, o = T.eq[:, 128 * b:128 * b + 128], T.ep[:, 128 * b:128 * b + 128], T.psb[:, 512 * b:512 * b + C]
-                mm(o, e, ep, T.qf[:, 0:C], T.pf[:, 0:C], True, False, ["eq%d" % b, "qf0", "qf1"], ["psb%d" % b])
-                mm(o, e, ep, lq[:, 0:C], lp[:, 0:C], False, True, ["eq%d" % b, "lq%d" % k], ["psb%d" % b])
+                mm(T.psb[:, 512 * b:512 * b + C], T.eq[:, 128 * b:128 * b + 128], T.ep[:, 128 * b:128 * b + 128], q[:, 0:C], p[:, 0:C], start, not start,
+                   ["eq%d" % b] + r, ["psb%d" % b])
 
-        def half(b):
-            act(T.fh[:, C * b:C * b + C], T.psa[:, 512 * b:512 * b + C], ["psa%d" % b], ["fh%d" % b], 0.5)
+        def meet(b, lo, hi):
+            act(T.zf[:, C * b + lo:C * b + hi], T.psb[:, 512 * b + lo:512 * b + hi], ["psb%d" % b], ["zf%d.%d" % (b, lo)], 0.5)
 
-        def meet(b):
-            act(T.zf[:, C * b:C * b + C], T.psb[:, 512 * b:512 * b + C], ["psb%d" % b], ["zf%d" % b], 0.5)
-
-        if k > 0:
-            quant_f(0)
-            quant_f(1)
-            meet_products()
-            for b in range(4):
-                half(b)
         op("v", lambda: V.tensor_tensor_scan(T.ts[:], sl[:], T.pk[:], 0.0, A.mult, A.add), ["sl%d" % k, "pk0", "pk1", "pk2"], ["ts"])
-        tcopy(T.t0[:, 0:16], T.ts[:, 1:48:3], ["ts"], ["t0"])
-        spare.append(lambda: tcopy(T.t0[:, 16:32], T.ts[:, 2:48:3], ["ts"], ["t0e"]))
+        tabs = {1: 0, "e": 16}
+        rows = {1: "w0", "A": "aa", "a": "ar"}
+        tcopy(T.tt[:, 0:16], T.ts[:, 1:48:3], ["ts"], ["tt1"])
+        hop(T.w0, "w0", T.wi[:, 0:512], ["wi"], T.tt, "tt1", 0, 8)
+        tcopy(T.tt[:, 16:32], T.ts[:, 2:48:3], ["ts"], ["tte"])
+        spare = {}
         if k == 0:
-            spare.append(lambda: quant_f(0))
-            spare.append(lambda: quant_f(1))
-            for n in ("st1", "st2"):
-                spare.append(lambda n=n: fill(T[n][:], -1.0, [n]))
-                spare.append(lambda n=n: fill(T[n][:, 0:48:3], 0.0, [n]))
-            spare.append(lambda: quant(T.vq[:, 0:128], T.vp[:, 0:128], T.vt[:, 0:512], ["vt"], ["vq"]))
-        hop(T.wa, "wa", T.wi[:, 0:512], ["wi"], T.t0, "t0", 0)
-        off, oname, c0, a = T.t0, "t0", 0, 0
-        for i in range(4):
-            for _ in range(3):
-                hop(win[1 - a], wn[1 - a], win[a][:, 0:512], [wn[a] + ".v", wn[a] + ".s", wn[a] + ".k"], off, oname, c0)
-                a = 1 - a
-            if i < 3:
-                if i == 0 and k == 0:
-                    meet_products()
-                    half(0)
-                    half(1)
-                if i == 1:
-                    meet(0)
-                    meet(1)
-                if i == 2:
-                    meet(2)
-                    if k == 0:
-                        meet(3)
-                scan(win[a], [wn[a] + ".v", wn[a] + ".s"])
-                table(T.tt[:, 16 * i:16 * i + 16], 256.25, ["tt%d" % i])
-                off, oname, c0 = T.tt, "tt%d" % i, 16 * i
-        hop(T.ar, "ar", win[a][:, 0:512], [wn[a] + ".v", wn[a] + ".s", wn[a] + ".k"], T.t0, "t0e", 16)
-        if k == 0:
-            act(T.fr[:], T.wi[:, C:2 * C].indirect(T.ft[:, 0:16]), ["wi", "ft"], ["fr"])
-        else:
-            meet(3)
-        scan(T.ar, ["ar.v", "ar.s"])
-        table(T.at[:], 0.25, ["at"])
+            spare = {2: lambda: fill(T.st1[:], -1.0, ["st1"]), 3: lambda: fill(T.st1[:, 0:48:3], 0.0, ["st1"]),
+                     5: lambda: fill(T.st2[:], -1.0, ["st2"]), 8: lambda: fill(T.st2[:, 0:48:3], 0.0, ["st2"]),
+                     "a": lambda: quant(T.vq[:, 0:128], T.vp[:, 0:128], T.vt[:, 0:512], ["vt"], ["vq"])}
+        pieces = {55: (0, 0, 128), 89: (0, 128, C), "A": (1, 0, 128), 178: (1, 128, C)}
+        for i, (tab, new, win, by) in enumerate(JUMPS):
+            if new not in rows:
+                rows[new] = "w%d" % ((len(rows) - 2) % 3)
+            w, o = rows[win], rows[new]
+            args = (T[o], o, T[w][:, 0:512], [w + ".v", w + ".s", w + ".k"], T.tt, "tt%s" % by, tabs[by], 8 if tab is None else 12)
+            hop_s(*args)
+            if tab is not None:
+                scan(T[rows[tab]], [rows[tab] + ".v", rows[tab] + ".s"], "sc%d" % (1 + i % 2))
+            hop_v(*args)
+            if tab is not None:
+                tabs[tab] = 16 * len(tabs)
+                table(T.tt[:, tabs[tab]:tabs[tab] + 16], 256.25, ["tt%s" % tab], "sc%d" % (1 + i % 2))
+            if new in spare:
+                spare[new]()
+            if new in pieces:
+                meet(*pieces[new])
+        meet(2, 0, C)
+        meet(3, 0, C)
+        scan(T.ar, ["ar.v", "ar.s"], "sc1")
+        table(T.at[:], 0.25, ["at"], "sc1")
 
-        def list_row():
-            act(rr[:], frow[:, 0:C].indirect(T.at[:, 0:16]), [frname, "at"], ["rr%d" % k])
-
-        def list_out():
-            table(rt[:], 0.25, ["rt%d" % k], "scr")
-            nd = T.cores[rank ^ ROUNDS[k + 1]]
-            send(nd, T["el%d" % (k + 1)][:], rt[:], "ar_l%d" % (k + 1), ["rt%d" % k])
-            arrives("ar_l%d" % (k + 1), len(topo.engines(nd, core)), ["el%d" % (k + 1)])
+        def list_row(out, name):
+            act(out[:], frow[:, 0:C].indirect(T.at[:, 0:16]), [frname, "at"], [name])
 
         def quant_z():
             for h in range(2):
@@ -325,47 +341,43 @@ def rank_program(g, core, T, topo):
                 quant(T.qz[:, c:c + 128], T.pz[:, c:c + 128], T.zt[:, 4 * c:4 * c + 512], ["zt%d" % b for b in range(4)], ["qz%d" % h])
 
         if k == 0:
-            list_row()
+            list_row(rr, "rr0")
         for b in range(4):
             f = tcopy if b == 0 else act
-            f(T.zt[:, b:1024:4], T.zf[:, C * b:C * b + C].indirect(T.at[:, 0:16]), ["zf%d" % b, "at"], ["zt%d" % b])
+            f(T.zt[:, b:1024:4], T.zf[:, C * b:C * b + C].indirect(T.at[:, 0:16]), ["zf%d.0" % b] + ["zf%d.128" % b] * (b < 2) + ["at"], ["zt%d" % b])
         if k == 0:
             scan(rr, ["rr%d" % k], "scr")
-            list_out()
+            list_out(k)
             tcopy(T.ir[:, 0:C].indirect(rt[:, 0:16]), T.wi[:, C:2 * C], ["wi", "rt%d" % k], ["ir"])
             quant_z()
-            scan(T.ir, ["ir"])
-            table(it[:], 0.25, ["it%d" % k])
+            scan(T.ir, ["ir"], "sc2")
         else:
             tcopy(T.ir[:, 0:C].indirect(T.at[:, 0:16]), T.wi[:, C:2 * C], ["wi", "at"], ["ir"])
             quant_z()
             hop(T.iv, "iv", T.ir[:, 0:C], ["ir"], T["it%d" % (k - 1)], "it%d" % (k - 1), 0, 12)
-            list_row()
-            scan(T.iv, ["iv.v", "iv.s"])
-            table(it[:], 0.25, ["it%d" % k])
-            if k < 2:
-                scan(rr, ["rr%d" % k], "scr")
+            scan(T.iv, ["iv.v", "iv.s"], "sc2")
+        table(it[:], 0.25, ["it%d" % k], "sc2")
         cuts = ((0, 0, 128, T.psb[:, 0:128], "psb0"), (0, 128, C, T.psa[:, 0:128], "psa0")) + tuple(
             (b, 0, C, T.psb[:, 512 * b:512 * b + C], "psb%d" % b) for b in (1, 2, 3))
         for b, lo, hi, o, n in cuts:
             mm(o, T.wq[:, 128 * b:128 * b + 128], T.wp[:, 128 * b:128 * b + 128], T.qz[:, lo:hi], T.pz[:, lo:hi], True, True,
                ["wq", "wp"] + ["qz%d" % h for h in range(2) if lo <= 128 * h < hi], [n])
         for b, lo, hi, o, n in cuts:
-            if k == 0 and b > 1:
-                half(b)
             act(T.pb[:, C * b + lo:C * b + hi], o, [n], ["pb%d.%d" % (b, lo)], 0.015625)
+        if k == 1:
+            list_row(rr, "rr1")
+        if k == 2:
+            list_row(T.lnf, "lnf")
         xn = T["xt%d" % (k + 1)]
-        for b in range(4):
-            ttt(xn[:, b:1024:4], T.pb[:, C * b:C * b + C].indirect(it[:, 0:16]), T.fh[:, C * b:C * b + C], A.add,
-                ["pb%d.%d" % (c, lo) for c, lo, hi, o, n in cuts if c == b] + ["it%d" % k, "fh%d" % b], ["xt%d.%d" % (k + 1, b)])
-            if b == 0 and k == 1:
-                list_out()
-    act(T.lnf[:], T.rr2[:], ["rr2"], ["lnf"])
+        for b, lo, hi in BACK[k == 2]:
+            ttt(xn[:, 4 * lo + b:4 * hi:4], T.pb[:, C * b:C * b + C].indirect(it[:, lo // 16:hi // 16]), T.fh[:, C * b + lo:C * b + hi], A.add,
+                ["pb%d.%d" % (c, l) for c, l, h, o, n in cuts if c == b] + ["it%d" % k, "fh%d" % b],
+                ["xt%d.%d.%d" % (k + 1, b, h) for h in range(2) if lo <= 128 * h < hi])
     op("y", lambda: g.sync.dma_start(T.ln[:], T.lnf[0:128:16, :]), ["lnf"], ["ln"], "out", 16)
     Q3 = ["qx3.0", "qx3.1"]
     for h in range(2):
         c = 128 * h
-        quant(T.qx3[:, c:c + 128], T.px3[:, c:c + 128], T.xt3[:, 4 * c:4 * c + 512], ["xt3.%d" % b for b in range(4)], [Q3[h]])
+        quant(T.qx3[:, c:c + 128], T.px3[:, c:c + 128], T.xt3[:, 4 * c:4 * c + 512], ["xt3.%d.%d" % (b, h) for b in range(4)], [Q3[h]])
         mm(T.psa[:, 4 * c:4 * c + 128], T.vq[:, 0:128], T.vp[:, 0:128], T.qx3[:, c:c + 128], T.px3[:, c:c + 128], True, True, ["vq", Q3[h]], ["psa%d" % h])
     op("y", lambda: g.sync.dma_start(T.oc[:, 0:4 * C], T.qx3[:, 0:C].bitcast(dt.uint8)), Q3, ["oc"], "out", 16)
 
@@ -382,3 +394,6 @@ def rank_program(g, core, T, topo):
     scales("s", S, 3)
     for s, n in sorted(total.items()):
         g.wait_ge(T.sem[s], n)
+
+
+BACK = (((0, 0, C), (1, 0, C), (2, 0, C), (3, 0, C)), ((0, 0, C), (1, 0, C), (2, 0, C), (3, 0, C)))

@@ -3,33 +3,45 @@ from concourse.mybir import dt, AluOpType, ActivationFunctionType
 C = 256
 ROUNDS = (1, 2, 4)
 COPY = ActivationFunctionType.Copy
+IDENTITY = ActivationFunctionType.Identity
 LIFT = 65536.0
 CODES = "float8_e4m3fn_x4"
 JUMPS = ((None, 2, 1, 1), (2, 3, 2, 1), (3, 5, 3, 2), (5, 8, 5, 3), (8, 13, 8, 5), (13, 21, 13, 8), (21, 34, 21, 13), (34, 55, 34, 21),
          (None, 89, 55, 34), (89, "A", 89, "e"), ("A", 178, 89, 89), (None, "a", 178, "A"))
+MEETS = {"A": (0, 0, 128), 178: (0, 128, C), "a": (1, 0, 128)}
+BACK = (("pick", 2, 0, 128), ("pick", 2, 128, C), ("both", 0, 0, C), ("list", 0, 0, 0), ("both", 1, 0, C), ("both", 3, 0, C), ("add", 2, 0, 128), ("add", 2, 128, C),
+        ("head", 0, 0, 128), ("head", 0, 128, C))
+LAST = BACK + (("store", "ln", 0, C), ("store", "oc", 0, C), ("store", "osc", 0, C), ("store", "yv", 0, 128), ("store", "ys", 128, C), ("store", "y", 0, C))
+OPT = {"back": (BACK, LAST), "rr": "M", "sg": (2,), "lays": ((3, 2, 1, 0), ("e", 3, 2, 1)), "late": (("k0", "k1", "k3", "q"), ("k0", "k1", "k3", "q")), "fld": True, "n1": 12, "direct": (1, 2), "iv": 12, "rcut": (128, 192),
+       "z": (("v", 0, 0, C), ("s", 1, 0, C), ("s", 2, 0, C), ("s", 3, 0, 128), ("s", 3, 128, C), ("v", None, 0, C))}
 
 SCRATCH = {
-    "flb": ("sbuf", [128, 16], "int32"),
-    "ft": ("sbuf", [128, 16], "uint16"), "f4": ("sbuf", [128, 64], "uint16"), "fr": ("sbuf", [128, C], "bfloat16"),
+    "fld": ("dram", [128, 16], "int32"), "flb": ("sbuf", [128, 16], "int32"), "ft": ("sbuf", [128, 16], "uint16"), "fi": ("sbuf", [128, 16], "uint16"), "fr": ("sbuf", [128, C], "bfloat16"),
     "ut": ("sbuf", [128, 512], "bfloat16"), "uq": ("sbuf", [128, 128], CODES), "up": ("sbuf", [128, 128], "uint8"),
     "urq": ("sbuf", [128, 128], CODES), "urp": ("sbuf", [128, 128], "uint8"),
     "vt": ("sbuf", [128, 512], "bfloat16"), "vq": ("sbuf", [128, 128], CODES), "vp": ("sbuf", [128, 128], "uint8"),
     "wq": ("sbuf", [128, 512], CODES), "wp": ("sbuf", [128, 512], "uint8"),
-    "one": ("sbuf", [128, 516], "bfloat16"),
     "ew": ("sbuf", [128, 516], "bfloat16"), "eq": ("sbuf", [128, 512], CODES), "ep": ("sbuf", [128, 512], "uint8"),
-    "xf": ("sbuf", [128, 1024], "bfloat16"), "qf": ("sbuf", [128, C], CODES), "pf": ("sbuf", [128, C], "uint8"),
     "zt": ("sbuf", [128, 1024], "bfloat16"), "qz": ("sbuf", [128, C], CODES), "pz": ("sbuf", [128, C], "uint8"),
-    "fh": ("sbuf", [128, 1024], "bfloat16"), "zf": ("sbuf", [128, 1024], "bfloat16"), "pb": ("sbuf", [128, 1024], "float32"),
-    "wi": ("sbuf", [128, 512], "bfloat16"),
-    "jm": ("sbuf", [128, C], "int32"), "jm2": ("sbuf", [128, C], "int32"),
-    "thr": ("sbuf", [128, C], "float32"), "rst": ("sbuf", [128, C], "bfloat16"), "cu": ("sbuf", [128, C], "bfloat16"),
-    "k1": ("sbuf", [128, C], "float32"), "sc0": ("sbuf", [128, 1], "float32"), "scc": ("sbuf", [128, 1], "float32"),
+    "fh": ("sbuf", [128, 1024], "bfloat16"), "zf": ("sbuf", [128, 1024], "bfloat16"),
+    "xf": ("sbuf", [128, 1024], "bfloat16"), "qf": ("sbuf", [128, C], CODES), "pf": ("sbuf", [128, C], "uint8"),
+    "f4": ("sbuf", [128, 64], "uint16"),
+    "pb": ("sbuf", [128, 1024], "float32"), "pg": ("sbuf", [128, C], "float32"),
+    "wi": ("sbuf", [128, 516], "bfloat16"), "wcol": ("sbuf", [128, 1], "float32"),
+    "jm": ("sbuf", [128, 16], "int32"), "jm2": ("sbuf", [128, 16], "int32"), "r16": ("sbuf", [128, 16], "float32"),
+    "k16": ("sbuf", [128, 16], "float32"), "c16": ("sbuf", [128, 16], "float32"), "po": ("sbuf", [128, 16], "uint16"),
+    "thr": ("sbuf", [128, C], "float32"), "cu": ("sbuf", [128, C], "bfloat16"), "rst": ("sbuf", [128, C], "bfloat16"),
+    "sc0": ("sbuf", [128, 1], "float32"), "scc": ("sbuf", [128, 1], "float32"),
     "pq": ("sbuf", [128, 16], "int32"), "pq2": ("sbuf", [128, 16], "int32"), "cj": ("sbuf", [128, 16], "float32"),
-    "jj": ("sbuf", [128, 16], "float32"), "jh": ("sbuf", [128, 16], "float32"), "oi": ("sbuf", [128, 8], "int32"), "ou": ("sbuf", [128, 8], "uint16"),
+    "jj": ("sbuf", [128, 16], "float32"), "jh": ("sbuf", [128, 16], "float32"),
+    "oi": ("sbuf", [128, 8], "int32"), "ou": ("sbuf", [128, 8], "uint16"),
     "mb": ("sbuf", [128, C], "bfloat16"), "ms": ("sbuf", [128, C], "bfloat16"),
     "sc1": ("sbuf", [128, C], "bfloat16"), "sc2": ("sbuf", [128, C], "bfloat16"), "scr": ("sbuf", [128, C], "bfloat16"),
     "eh": ("sbuf", [128, 16], "float32"), "ed": ("sbuf", [128, 16], "float32"),
-    "pk": ("sbuf", [128, 48], "float32"), "ts": ("sbuf", [128, 48], "float32"),
+    "pk": ("sbuf", [128, 48], "float32"), "ts": ("sbuf", [128, 64], "float32"),
+    "d0": ("sbuf", [128, 64], "float32"), "d1": ("sbuf", [128, 64], "float32"), "sb": ("sbuf", [128, 16], "float32"), "ch": ("sbuf", [128, 16], "float32"),
+    "co": ("sbuf", [128, 16], "uint16"), "q2": ("sbuf", [128, 1], "float32"), "c2": ("sbuf", [128, C], "bfloat16"),
+    "ea": ("sbuf", [128, 512], "bfloat16"), "eb": ("sbuf", [128, 512], "bfloat16"), "wd": ("sbuf", [128, 512], "bfloat16"),
     "tt": ("sbuf", [128, 16 * 12], "uint16"),
     "w0": ("sbuf", [128, 512], "bfloat16"), "w1": ("sbuf", [128, 512], "bfloat16"), "w2": ("sbuf", [128, 512], "bfloat16"),
     "aa": ("sbuf", [128, C], "bfloat16"), "ar": ("sbuf", [128, C], "bfloat16"), "at": ("sbuf", [128, 16], "uint16"),
@@ -47,10 +59,12 @@ for _k in range(3):
     SCRATCH["lp%d" % _k] = ("sbuf", [128, C], "uint8")
     SCRATCH["st%d" % _k] = ("sbuf", [128, 48], "bfloat16")
     SCRATCH["sl%d" % _k] = ("sbuf", [128, 48], "bfloat16")
+    SCRATCH["su%d" % _k] = ("sbuf", [128, 16], "uint16")
+    SCRATCH["sv%d" % _k] = ("sbuf", [128, 16], "uint16")
     SCRATCH["rr%d" % _k] = ("sbuf", [128, C], "bfloat16")
     SCRATCH["rt%d" % _k] = ("sbuf", [128, 16], "uint16")
     SCRATCH["it%d" % _k] = ("sbuf", [128, 16], "uint16")
-SEMAPHORES = (["cv", "cs", "cp", "cg", "lo", "lf", "lx", "lu", "lv", "lw", "lws", "out"]
+SEMAPHORES = (["cv", "cs", "cp", "cg", "lo", "ld", "lf", "lx", "lu", "lv", "lw", "lws", "out"]
               + ["%s%d" % (a, k) for a in ("ar_s", "ar_l", "ar_d") for k in range(3)])
 
 
@@ -141,7 +155,7 @@ def rank_program(g, core, T, topo):
         else:
             op("s", lambda: S.activation(out, in_, COPY, scale=scale), r, w)
 
-    def mm(out, a, ap, b, bp, start, stop, r, w):
+    def mm(out, a, ap, b, bp, r, w, start=True, stop=True):
         op("p", lambda: P.matmul_mx(out, a, ap, b, bp, start, stop), r, w)
 
     def iota(out, pattern, base, cm, w, small=False):
@@ -168,44 +182,104 @@ def rank_program(g, core, T, topo):
         hop_s(*a)
         hop_v(*a)
 
-    op("s", lambda: S.dma_start(T.flb[:], T.fl[:]), [], ["flb"], "lf", 16)
+    if OPT["fld"]:
+        op("s", lambda: S.dma_start(T.fld[:], T.fl[:]), [], ["fld"], "ld", 16)
+    else:
+        op("s", lambda: S.dma_start(T.flb[:], T.fl[:]), [], ["flb"], "lf", 16)
     op("y", lambda: g.sync.dma_start(T.ut[:], T.u[:]), [], ["ut"], "lu", 16)
     op("y", lambda: g.sync.dma_start(T.xt0[:], T.x[:]), [], ["xt0.%d.%d" % (b, h) for b in range(4) for h in range(2)], "lx", 16)
-    iota(T.jm[:], [[1, C]], 0, -1, ["jm"])
-    iota(T.oi[:], [[16, 8]], 0, 0, ["oi"])
-    iota(T.wi[:], [[1, 512]], -C, 0, ["wi"], True)
+    if OPT["fld"]:
+        op("y", lambda: g.sync.dma_start(T.flb[:], T.fl[:]), [], ["flb"], "lf", 16)
+    iota(T.jm[:], [[1, 16]], 0, -1, ["jm"])
     iota(T.pq[:], [[0, 16]], 0, 1, ["pq"])
+    iota(T.wcol[:], [[0, 1]], 3 - C, 4, ["wcol"], True)
+    iota(T.wi[:], [[1, 516]], -C, 0, ["wi"], True)
+    iota(T.oi[:], [[16, 8]], 0, 0, ["oi"])
     iota(T.cj[:], [[16, 16]], C, 0, ["cj"], True)
     first = T.cores[rank ^ ROUNDS[0]]
-    send(first, T.el0[:], T.flb[:], "ar_l0", ["flb"])
+    if OPT["fld"]:
+        send(first, T.el0[:], T.fld[:], "ar_l0", ["fld"])
+    else:
+        send(first, T.el0[:], T.flb[:], "ar_l0", ["flb"])
     arrives("ar_l0", len(topo.engines(first, core)), ["el0"])
-    fill(T.one[:], 1.0, ["one"])
     fill(T.st0[:], -1.0, ["st0"])
-    op("g", lambda: g.affine_select(T.ew[:], T.one[:], [[1, 516]], A.is_equal, 0.0, -4, -4), ["one"], ["ew"])
-    fill(T.st0[:, 0:48:3], 0.0, ["st0"])
+    fill(T.d0[:], -1.0, ["d0"])
+    iota(T.w0[:, C:2 * C], [[1, C]], 0, 0, ["w0.k"], True)
     tts(T.jm2[:], T.jm[:], 15, None, A.bitwise_and, None, ["jm"], ["jm2"])
-    tcopy(T.ou[:], T.oi[:], ["oi"], ["ou"])
-    tts(T.rst[:], T.jm2[:], 0.0, None, A.not_equal, None, ["jm2"], ["rst"])
-    tts(T.k1[:], T.jm2[:], 1.0, LIFT - 1.0, A.is_equal, A.mult, ["jm2"], ["k1"])
-    act(T.thr[:], T.rst[:], ["rst"], ["thr"], 1.0e29)
-    tts(T.sc0[:], T.jm2[:, 15:16], 0.0, 1.0 - 1.0 / LIFT, A.is_equal, A.mult, ["jm2"], ["sc0"])
-    ttt(T.cu[:], T.k1[:], T.rst[:], A.add, ["k1", "rst"], ["cu"])
-    tts(T.scc[:], T.sc0[:], 1.0 / LIFT, None, A.add, None, ["sc0"], ["scc"])
-    tcopy(T.ft[:], T.flb[:], ["flb"], ["ft"])
     tts(T.pq2[:], T.pq[:], 15, None, A.bitwise_and, None, ["pq"], ["pq2"])
-    for n in ("w0", "w1", "w2"):
-        act(T[n][:, C:2 * C], T.wi[:, C:2 * C], ["wi"], [n + ".k"])
-    quant(T.uq[:, 0:128], T.up[:, 0:128], T.ut[:, 0:512], ["ut"], ["uq"])
+    fill(T.st0[:, 0:48:3], 0.0, ["st0"])
+    fill(T.d0[:, 0:64:4], 0.0, ["d0"])
+    tts(T.r16[:], T.jm2[:], 0.0, None, A.not_equal, None, ["jm2"], ["r16"])
+    tts(T.k16[:], T.jm2[:], 1.0, LIFT - 1.0, A.is_equal, A.mult, ["jm2"], ["k16"])
+    tcopy(T.po[:], T.pq2[:], ["pq2"], ["po"])
+    tts(T.sc0[:], T.jm2[:, 15:16], 0.0, 1.0 - 1.0 / LIFT, A.is_equal, A.mult, ["jm2"], ["sc0"])
+    ttt(T.c16[:], T.k16[:], T.r16[:], A.add, ["k16", "r16"], ["c16"])
+    tts(T.scc[:], T.sc0[:], 1.0 / LIFT, None, A.add, None, ["sc0"], ["scc"])
+    act(T.rst[:], T.r16[:, 0:16].indirect(T.po[:, 0:16]), ["r16", "po"], ["rst"])
+    act(T.cu[:], T.c16[:, 0:16].indirect(T.po[:, 0:16]), ["c16", "po"], ["cu"])
+    act(T.thr[:], T.rst[:], ["rst"], ["thr"], 1.0e29)
+    tts(T.ew[:], T.wi[:], T.wcol[:, 0:1], 0.5, A.is_equal, A.mult, ["wi", "wcol"], ["ew"])
+
+    def own_list():
+        tcopy(T.ft[:], T.flb[:], ["flb"], ["ft"])
+
+    def own_row():
+        act(T.fr[:], T.wi[:, C:2 * C].indirect(T.ft[:, 0:16]), ["wi", "ft"], ["fr"])
+
+    if not OPT["fld"]:
+        own_list()
+
+    def quant_e(b):
+        quant(T.eq[:, 128 * b:128 * b + 128], T.ep[:, 128 * b:128 * b + 128], T.ew[:, 3 - b:515 - b], ["ew"], ["eq%d" % b])
+
+    def four(name, b):
+        tts(T.f4[:, 16 * b:16 * b + 16], T[name][:], 4.0, float(b), A.mult, A.add, [name], ["f4.%d" % b])
+
+    tcopy(T.ou[:], T.oi[:], ["oi"], ["ou"])
     ttt(T.jj[:], T.pq2[:], T.cj[:], A.add, ["pq2", "cj"], ["jj"])
+    quant_e(0)
+    tts(T.jh[:], T.jj[:], 0.5, None, A.mult, None, ["jj"], ["jh"])
+    quant_e(1)
+    quant(T.uq[:, 0:128], T.up[:, 0:128], T.ut[:, 0:512], ["ut"], ["uq"])
+    quant_e(2)
     op("v", lambda: V.tensor_copy(T.urq[:, 0:128].bitcast(dt.uint32), T.uq[:, 0:128].bitcast(dt.uint32).indirect(T.ou[:, 0:8])), ["uq", "ou"], ["urq"])
     act(T.urp[:, 0:128], T.up[:, 0:128].indirect(T.ou[:, 0:8]), ["uq", "ou"], ["urp"])
-    act(T.fr[:], T.wi[:, C:2 * C].indirect(T.ft[:, 0:16]), ["wi", "ft"], ["fr"])
+    if not OPT["fld"]:
+        own_row()
+        for b in (3, 2, 1, 0):
+            four("flb", b)
+    else:
+        quant_e(3)
+    laid_by = []
+    consts = {21: lambda: (fill(T.d0[:, 1:64:4], 4.0, ["d0"]), tts(T.q2[:], T.pq2[:, 0:1], 2.0, None, A.mult, None, ["pq2"], ["q2"])),
+              34: lambda: (tts(T.co[:], T.cj[:], -128.0, None, A.add, None, ["cj"], ["co"]), tts(T.ch[:], T.jj[:], 2.0, 0.5 - 3 * C, A.mult, A.add, ["jj"], ["ch"])),
+              55: lambda: tts(T.d1[:, 1:64:4], T.jj[:], -8.0, 8.0 * C - 2.0, A.mult, A.add, ["jj"], ["d1.1"])}
 
-    def four(src, name, b):
-        tts(T.f4[:, 16 * b:16 * b + 16], src[:], 4.0, float(b), A.mult, A.add, [name], ["f4.%d" % b])
+    def head(k, h):
+        c = 128 * h
+        q, p, name = T["qx%d" % k], T["px%d" % k], "qx%d.%d" % (k, h)
+        quant(q[:, c:c + 128], p[:, c:c + 128], T["xt%d" % k][:, 4 * c:4 * c + 512], ["xt%d.%d.%d" % (k, b, h) for b in range(4)], [name])
+        a, ap, r = (T.urq, T.urp, ["urq", "urp"]) if k < 3 else (T.vq, T.vp, ["vq"])
+        mm(T.psb[:, 4 * c:4 * c + 128], a[:, 0:128], ap[:, 0:128], q[:, c:c + 128], p[:, c:c + 128], r + [name], ["psb%d" % h])
 
-    for b in range(4):
-        four(T.ft, "ft", b)
+    def store(what, hs):
+        lo, hi = 128 * hs[0], 128 * hs[-1] + 128
+        Q3 = ["qx3.%d" % h for h in hs]
+        if what == "ln":
+            act(T.lnf[:], T.rr1[:, 0:C].indirect(T.at[:, 0:16]), ["rr1a", "rr1b", "rr1c", "at"], ["lnf"])
+            op("y", lambda: g.sync.dma_start(T.ln[:], T.lnf[0:128:16, :]), ["lnf"], ["ln"], "out", 16)
+        if what == "oc":
+            op("y", lambda: g.sync.dma_start(T.oc[:, 4 * lo:4 * hi], T.qx3[:, lo:hi].bitcast(dt.uint8)), Q3, ["oc%d" % lo], "out", 16)
+        if what == "osc":
+            for i in range(4):
+                op("y", lambda i=i: g.sync.dma_start(T.osc[4 * i:4 * i + 4, 0:C], T.px3[32 * i:32 * i + 4, 0:C]), Q3, ["osc%d" % i], "out", 16)
+        if what in ("yv", "ys"):
+            (tcopy if what == "yv" else act)(T.yb[:, lo:hi], T.psb[:, 4 * lo:4 * lo + 128], ["psb%d" % hs[0]], ["y%d" % hs[0]])
+        if what == "y":
+            op("s", lambda: S.dma_start(T.y[:, lo:hi], T.yb[:, lo:hi]), ["y%d" % h for h in hs], ["yo%d" % lo], "out", 16)
+
+    head(0, 0)
+    head(0, 1)
 
     for k, m in enumerate(ROUNDS):
         d = T.cores[rank ^ m]
@@ -215,7 +289,23 @@ def rank_program(g, core, T, topo):
         rr, rt, it = T["rr%d" % k], T["rt%d" % k], T["it%d" % k]
         Xt = ["xt%d.%d.%d" % (k, b, h) for b in range(4) for h in range(2)]
         Qx = ["qx%d.0" % k, "qx%d.1" % k]
-        frow, frname = (T.fr, "fr") if k == 0 else (T["rr%d" % (k - 1)], "rr%d" % (k - 1))
+        frow, ftab, finv = ("fr", "ft", "fi") if k == 0 else ("rr%d" % (k - 1), "rt%d" % (k - 1), "it%d" % (k - 1))
+        Fr = ["fr"] if k == 0 else [frow + x for x in "abc"]
+
+        def unpack(ps, name, q, p, r, start=True, stop=True):
+            for b in range(4):
+                mm(ps[:, 512 * b:512 * b + C], T.eq[:, 128 * b:128 * b + 128], T.ep[:, 128 * b:128 * b + 128], q[:, 0:C], p[:, 0:C], ["eq%d" % b] + r, [name + str(b)],
+                   start, stop)
+
+        def keep(b, lo, hi):
+            act(T.fh[:, C * b + lo:C * b + hi], T.psa[:, 512 * b + lo:512 * b + hi], ["psa%d" % b], ["fh%d.%d" % (b, c) for c in (0, 128) if lo <= c < hi])
+
+        def lay(f, b):
+            f(T.xf[:, b:1024:4], xt[:, 0:1024].indirect(T.f4[:, 16 * b:16 * b + 16]), Xt + ["f4.%d" % b], ["xf%d" % b])
+
+        def quant_f(h):
+            c = 128 * h
+            quant(T.qf[:, c:c + 128], T.pf[:, c:c + 128], T.xf[:, 4 * c:4 * c + 512], ["xf%d" % b for b in range(4)], ["qf%d" % h])
 
         def list_out(k):
             table(T["rt%d" % k][:], 0.25, ["rt%d" % k], "scr")
@@ -223,99 +313,148 @@ def rank_program(g, core, T, topo):
             send(nd, T["el%d" % (k + 1)][:], T["rt%d" % k][:], "ar_l%d" % (k + 1), ["rt%d" % k])
             arrives("ar_l%d" % (k + 1), len(topo.engines(nd, core)), ["el%d" % (k + 1)])
 
-        def lay(f, b):
-            f(T.xf[:, b:1024:4], xt[:, 0:1024].indirect(T.f4[:, 16 * b:16 * b + 16]), Xt + ["f4.%d" % b], ["xf%d" % b])
-
-        gaps = []
-        if k == 2:
-            gaps = [lambda: scan(frow, [frname], "scr"), lambda: list_out(k - 1)]
-        if k > 0:
-            gaps += [lambda b=b: four(T["rt%d" % (k - 1)], "rt%d" % (k - 1), b) for b in (2, 3, 0, 1)]
-
-        def gap(n=1):
-            for _ in range(n):
-                if gaps:
-                    gaps.pop(0)()
-
-        for h in range(2):
-            c = 128 * h
-            quant(qx[:, c:c + 128], px[:, c:c + 128], xt[:, 4 * c:4 * c + 512], Xt[h::2], [Qx[h]])
-            mm(T.psb[:, 4 * c:4 * c + 128], T.urq[:, 0:128], T.urp[:, 0:128], qx[:, c:c + 128], px[:, c:c + 128], True, True, ["urq", "urp", Qx[h]], ["psb%d" % h])
-        gap()
         if k == 0:
-            for b in (1, 2, 3):
-                lay(act, b)
+            gaps = [[lambda: quant_e(3)], [], [], [], []]
+            if OPT["fld"]:
+                gaps = [[lambda b=b: four("flb", b) for b in (3, 2, 1, 0)], [], [own_list], [], []]
+        elif OPT["rr"] == "D":
+            gaps = [[lambda b=b: four(ftab, b) for b in (1, 0)], [], [], [], []]
+        elif OPT["rr"] == "M":
+            gaps = [[lambda b=b: four(ftab, b) for b in (3, 2, 1, 0)], [], [], [], []]
+        else:
+            gaps = [[lambda: scan(T[frow], Fr, "scr")], [lambda: list_out(k - 1)], [lambda: four(ftab, 3)], [lambda: four(ftab, 2), lambda: four(ftab, 1)], [lambda: four(ftab, 0)]]
+        laid = []
+        direct = k in OPT["direct"]
+        if direct:
+            st, sl = T["su%d" % k], T["sv%d" % k]
+
+        def gap(i):
+            for f in gaps[i]:
+                f()
+            for b in OPT["lays"][k > 0]:
+                if b == "e":
+                    if b not in laid and direct:
+                        act(T.ea[:, 0:512:2], T.wi[:, 0:C].indirect(el[:, 0:16]), ["wi", "el%d" % k], ["ea.e"])
+                        laid.append(b)
+                elif b not in laid and wrote["f4.%d" % b] not in laid_by:
+                    lay(act, b)
+                    laid.append(b)
+                    laid_by.append(wrote["f4.%d" % b])
+
+        gap(0)
         for h in range(2):
             c = 128 * h
             ttt(T.mb[:, c:c + 128], T.psb[:, 4 * c:4 * c + 128], T.thr[:, c:c + 128], A.is_gt, ["psb%d" % h, "thr"], ["mb%d" % h])
-            gap(1 - h)
+            if h == 0:
+                gap(1)
         for h in range(2):
-            op("v", lambda c=128 * h: V.tensor_tensor_scan(T.ms[:, c:c + 128], T.rst[:, c:c + 128], T.mb[:, c:c + 128], 0.0, A.mult, A.add),
-               ["rst", "mb%d" % h], ["ms%d" % h])
-            gap(1 + h)
-        tts(st[:, 1:48:3], T.ms[:, 15:C:16], 2.0, -1.0, A.mult, A.add, ["ms0", "ms1"], ["st%d" % k])
+            c = 128 * h
+            if direct:
+                op("v", lambda: V.tensor_tensor_scan(T.ms[:, c:c + 128], T.c2[:, c:c + 128], T.mb[:, c:c + 128], -1000.0, A.max, A.add), ["c2", "mb%d" % h], ["ms%d" % h])
+            else:
+                op("v", lambda: V.tensor_tensor_scan(T.ms[:, c:c + 128], T.rst[:, c:c + 128], T.mb[:, c:c + 128], 0.0, A.mult, A.add), ["rst", "mb%d" % h], ["ms%d" % h])
+            gap(2 + h)
+        if direct:
+            tts(st[:], T.ms[:, 15:C:16], float(C), None, A.add, None, ["ms0", "ms1"], ["st%d" % k])
+        else:
+            tts(st[:, 1:48:3], T.ms[:, 15:C:16], 2.0, -1.0, A.mult, A.add, ["ms0", "ms1"], ["st%d" % k])
         send(d, sl[:], st[:], "ar_s%d" % k, ["st%d" % k])
         arrives("ar_s%d" % k, ne, ["sl%d" % k])
         send(d, lq[:, 0:C].bitcast(dt.uint8), qx[:, 0:C].bitcast(dt.uint8), "ar_d%d" % k, Qx)
         send(d, lp[:, 0:C], px[:, 0:C], "ar_d%d" % k, Qx)
         arrives("ar_d%d" % k, 2 * ne, ["lq%d" % k])
-        gap(4)
         if k == 0:
             wait("y", [wrote["sl0"]])
             op("y", lambda: g.sync.dma_start(T.wq[:, 0:512].bitcast(dt.uint8), T.wc[:]), [], ["wq"], "lw", 16)
             op("y", lambda: g.sync.dma_start(T.wp[:, 0:512], T.ws[:]), [], ["wp"], "lws", 16)
             op("y", lambda: g.sync.dma_start(T.vt[:], T.v[:]), [], ["vt"], "lv", 16)
-            for b in range(4):
-                quant(T.eq[:, 128 * b:128 * b + 128], T.ep[:, 128 * b:128 * b + 128], T.ew[:, 4 - b:516 - b], ["ew"], ["eq%d" % b])
-            tts(T.jh[:], T.jj[:], 0.5, None, A.mult, None, ["jj"], ["jh"])
-            lay(tcopy, 0)
-        else:
-            for b in (2, 3):
-                lay(act, b)
-            for b in (0, 1):
+        gap(4)
+        unpack(T.psa, "psa", qx, px, Qx)
+        if k == 0:
+            for n in ("w1", "w2"):
+                iota(T[n][:, C:2 * C], [[1, C]], 0, 0, [n + ".k"], True)
+            iota(T.ea[:, 1:512:2], [[1, C]], 0, 0, ["ea.k"], True)
+            iota(T.eb[:, 0:512:2], [[1, C]], 0, 0, ["eb.k"], True)
+        if direct:
+            ttt(T.sb[:], T.ms[:, 15:C:16], T.ch[:], A.subtract, ["ms0", "ms1", "ch"], ["sb"])
+            tts(T.eh[:], el[:], 0.5, None, A.mult, None, ["el%d" % k], ["eh"])
+            tcopy(T.eb[:, 1:512:2], T.ea[:, 0:512:2], ["ea.e"], ["eb.e"])
+            ttt(T.ed[:], T.eh[:], T.jh[:], A.subtract, ["eh", "jh"], ["ed"])
+            ttt(T.d1[:, 2:64:4], T.eh[:], T.jh[:], A.add, ["eh", "jh"], ["d1.2"])
+            tcopy(T.wd[:, 0:512:2], T.ea[:, 0:512].indirect(st[:, 0:16]), ["ea.e", "ea.k", "st%d" % k], ["wd0"])
+            act(T.wd[:, 1:512:2], T.eb[:, 0:512].indirect(st[:, 0:16]), ["eb.e", "eb.k", "st%d" % k], ["wd1"])
+            ttt(T.d0[:, 2:64:4], T.ed[:], T.sb[:], A.mult, ["ed", "sb", "d0"], ["d0.2"])
+            tts(T.d1[:, 3:64:4], T.d1[:, 2:64:4], 2.0, None, A.mult, None, ["d1.2"], ["d1.3"])
+        for b in range(4):
+            if b not in laid:
                 lay(tcopy, b)
+                laid_by.append(wrote["f4.%d" % b])
+        late = OPT["late"][k > 0]
+        late_s, late_v = [], []
+        if k == 0 and OPT["fld"]:
+            own_row()
         for b in range(4):
-            mm(T.psa[:, 512 * b:512 * b + C], T.eq[:, 128 * b:128 * b + 128], T.ep[:, 128 * b:128 * b + 128], qx[:, 0:C], px[:, 0:C], True, True,
-               ["eq%d" % b] + Qx, ["psa%d" % b])
-        for b in range(4):
-            act(T.fh[:, C * b:C * b + C], T.psa[:, 512 * b:512 * b + C], ["psa%d" % b], ["fh%d" % b], 0.5)
+            if b not in OPT["sg"]:
+                if "k%d" % b not in late:
+                    keep(b, 0, C)
+                else:
+                    late_s += [lambda b=b: keep(b, 0, 128), lambda b=b: keep(b, 128, C)]
 
-        def quant_f(h):
-            c = 128 * h
-            quant(T.qf[:, c:c + 128], T.pf[:, c:c + 128], T.xf[:, 4 * c:4 * c + 512], ["xf%d" % b for b in range(4)], ["qf%d" % h])
+        def meet_products():
+            unpack(T.psb, "psb", T.qf, T.pf, ["qf0", "qf1"], True, False)
+            unpack(T.psb, "psb", lq, lp, ["lq%d" % k], False, True)
 
-        tts(T.eh[:], el[:], 0.5, None, A.mult, None, ["el%d" % k], ["eh"])
-        quant_f(0)
-        ttt(T.ed[:], T.eh[:], T.jh[:], A.subtract, ["eh", "jh"], ["ed"])
-        ttt(T.pk[:, 1:48:3], T.eh[:], T.jh[:], A.add, ["eh", "jh"], ["pk1"])
-        quant_f(1)
-        ttt(T.pk[:, 0:48:3], T.ed[:], st[:, 1:48:3], A.mult, ["ed", "st%d" % k], ["pk0"])
-        tts(T.pk[:, 2:48:3], T.pk[:, 1:48:3], 2.0, None, A.mult, None, ["pk1"], ["pk2"])
-        for q, p, r, start in ((T.qf, T.pf, ["qf0", "qf1"], True), (lq, lp, ["lq%d" % k], False)):
-            for b in range(4):
-                mm(T.psb[:, 512 * b:512 * b + C], T.eq[:, 128 * b:128 * b + 128], T.ep[:, 128 * b:128 * b + 128], q[:, 0:C], p[:, 0:C], start, not start,
-                   ["eq%d" % b] + r, ["psb%d" % b])
+        if direct:
+            if "q" not in late:
+                quant_f(0)
+                quant_f(1)
+            else:
+                late_v += [lambda: quant_f(0), lambda: (quant_f(1), meet_products())]
+        else:
+            tts(T.eh[:], el[:], 0.5, None, A.mult, None, ["el%d" % k], ["eh"])
+            if k == 0:
+                tcopy(T.ir[:, 0:C].indirect(T.ft[:, 0:8]), T.wi[:, C:C + 128], ["wi", "ft"], ["ir"])
+            if "q" not in late:
+                quant_f(0)
+            ttt(T.ed[:], T.eh[:], T.jh[:], A.subtract, ["eh", "jh"], ["ed"])
+            ttt(T.pk[:, 1:48:3], T.eh[:], T.jh[:], A.add, ["eh", "jh"], ["pk1"])
+            if k == 0:
+                tcopy(T.ir[:, 0:C].indirect(T.ft[:, 8:16]), T.wi[:, C + 128:2 * C], ["wi", "ft"], ["ir"])
+            if "q" not in late:
+                quant_f(1)
+            else:
+                late_v += [lambda: quant_f(0), lambda: (quant_f(1), meet_products())]
+            ttt(T.pk[:, 0:48:3], T.ed[:], st[:, 1:48:3], A.mult, ["ed", "st%d" % k], ["pk0"])
+            tts(T.pk[:, 2:48:3], T.pk[:, 1:48:3], 2.0, None, A.mult, None, ["pk1"], ["pk2"])
+        if not late_v:
+            meet_products()
 
-        def meet(b, lo, hi):
-            act(T.zf[:, C * b + lo:C * b + hi], T.psb[:, 512 * b + lo:512 * b + hi], ["psb%d" % b], ["zf%d.%d" % (b, lo)], 0.5)
+        def meet(f, b, lo, hi):
+            f(T.zf[:, C * b + lo:C * b + hi], T.psb[:, 512 * b + lo:512 * b + hi], ["psb%d" % b], ["zf%d.%d" % (b, c) for c in (0, 128) if lo <= c < hi])
 
-        op("v", lambda: V.tensor_tensor_scan(T.ts[:], sl[:], T.pk[:], 0.0, A.mult, A.add), ["sl%d" % k, "pk0", "pk1", "pk2"], ["ts"])
         tabs = {1: 0, "e": 16}
         rows = {1: "w0", "A": "aa", "a": "ar"}
-        tcopy(T.tt[:, 0:16], T.ts[:, 1:48:3], ["ts"], ["tt1"])
-        hop(T.w0, "w0", T.wi[:, 0:512], ["wi"], T.tt, "tt1", 0, 8)
-        tcopy(T.tt[:, 16:32], T.ts[:, 2:48:3], ["ts"], ["tte"])
-        spare = {}
-        if k == 0:
-            spare = {2: lambda: fill(T.st1[:], -1.0, ["st1"]), 3: lambda: fill(T.st1[:, 0:48:3], 0.0, ["st1"]),
-                     5: lambda: fill(T.st2[:], -1.0, ["st2"]), 8: lambda: fill(T.st2[:, 0:48:3], 0.0, ["st2"]),
-                     "a": lambda: quant(T.vq[:, 0:128], T.vp[:, 0:128], T.vt[:, 0:512], ["vt"], ["vq"])}
-        pieces = {55: (0, 0, 128), 89: (0, 128, C), "A": (1, 0, 128), 178: (1, 128, C)}
+        if direct:
+            args = (T.w0, "w0", T.wd[:, 0:512], ["wd0", "wd1"], sl, "sl%d" % k, 0, OPT["n1"])
+            hop_s(*args)
+            tcopy(T.d1[:, 0:64:4], sl[:], ["sl%d" % k], ["d1.0"])
+            if OPT["n1"] < 16:
+                hop_v(*args)
+            else:
+                wrote["w0.v"] = wrote["w0.s"]
+            op("v", lambda: V.tensor_tensor_scan(T.ts[:], T.d0[:], T.d1[:], 0.0, A.mult, A.add), ["d0", "d0.2"] + ["d1.%d" % i for i in range(4)], ["ts"])
+            tcopy(T.tt[:, 0:16], T.ts[:, 2:64:4], ["ts"], ["tt1"])
+            tcopy(T.tt[:, 16:32], T.ts[:, 3:64:4], ["ts"], ["tte"])
+        else:
+            op("v", lambda: V.tensor_tensor_scan(T.ts[:, 0:48], sl[:], T.pk[:], 0.0, A.mult, A.add), ["sl%d" % k, "pk0", "pk1", "pk2"], ["ts"])
+            tcopy(T.tt[:, 0:16], T.ts[:, 1:48:3], ["ts"], ["tt1"])
+            hop(T.w0, "w0", T.wi[:, 0:512], ["wi"], T.tt, "tt1", 0, 8)
+            tcopy(T.tt[:, 16:32], T.ts[:, 2:48:3], ["ts"], ["tte"])
         for i, (tab, new, win, by) in enumerate(JUMPS):
             if new not in rows:
                 rows[new] = "w%d" % ((len(rows) - 2) % 3)
             w, o = rows[win], rows[new]
-            args = (T[o], o, T[w][:, 0:512], [w + ".v", w + ".s", w + ".k"], T.tt, "tt%s" % by, tabs[by], 8 if tab is None else 12)
+            args = (T[o], o, T[w][:, 0:512], [w + ".v", w + ".s", w + ".k"], T.tt, "tt%s" % by, tabs[by], 8 if tab is None else 10)
             hop_s(*args)
             if tab is not None:
                 scan(T[rows[tab]], [rows[tab] + ".v", rows[tab] + ".s"], "sc%d" % (1 + i % 2))
@@ -323,77 +462,84 @@ def rank_program(g, core, T, topo):
             if tab is not None:
                 tabs[tab] = 16 * len(tabs)
                 table(T.tt[:, tabs[tab]:tabs[tab] + 16], 256.25, ["tt%s" % tab], "sc%d" % (1 + i % 2))
-            if new in spare:
-                spare[new]()
-            if new in pieces:
-                meet(*pieces[new])
-        meet(2, 0, C)
-        meet(3, 0, C)
+            if late_s and tab is not None:
+                late_s.pop(0)()
+            if late_v and tab is not None:
+                late_v.pop(0)()
+            if k == 0 and new in consts:
+                consts[new]()
+            if k == 0 and new == 8:
+                scan(T.ir, ["ir"], "scr")
+            if k == 0 and new == 13:
+                table(T.fi[:], 0.25, ["fi"], "scr")
+            if k == 1 and new == 13:
+                quant(T.vq[:, 0:128], T.vp[:, 0:128], T.vt[:, 0:512], ["vt"], ["vq"])
+            if new in MEETS:
+                meet(tcopy, *MEETS[new])
+        meet(act, 2, 0, C)
+        meet(act, 3, 0, C)
         scan(T.ar, ["ar.v", "ar.s"], "sc1")
+        meet(tcopy, 1, 128, C)
         table(T.at[:], 0.25, ["at"], "sc1")
 
-        def list_row(out, name):
-            act(out[:], frow[:, 0:C].indirect(T.at[:, 0:16]), [frname, "at"], [name])
+        def list_row(f, lo, hi, name):
+            if k < 2:
+                f(rr[:, lo:hi], T[frow][:, 0:C].indirect(T.at[:, lo // 16:hi // 16]), Fr + ["at"], ["rr%d%s" % (k, name)])
 
-        def quant_z():
+        zw = [[], []]
+        for i, (e, b, lo, hi) in enumerate(OPT["z"]):
+            if b is None:
+                tcopy(T.ir[:, 0:C].indirect(T.at[:, lo // 16:hi // 16]), T.wi[:, C + lo:C + hi], ["wi", "at"], ["ir"])
+                continue
+            (tcopy if e == "v" else act)(T.zt[:, 4 * lo + b:4 * hi:4], T.zf[:, C * b:C * b + C].indirect(T.at[:, lo // 16:hi // 16]),
+                                         ["zf%d.0" % b, "zf%d.128" % b, "at", "qzr"][:3], ["zt%d.%d" % (b, lo)])
             for h in range(2):
-                c = 128 * h
-                quant(T.qz[:, c:c + 128], T.pz[:, c:c + 128], T.zt[:, 4 * c:4 * c + 512], ["zt%d" % b for b in range(4)], ["qz%d" % h])
-
-        if k == 0:
-            list_row(rr, "rr0")
-        for b in range(4):
-            f = tcopy if b == 0 else act
-            f(T.zt[:, b:1024:4], T.zf[:, C * b:C * b + C].indirect(T.at[:, 0:16]), ["zf%d.0" % b] + ["zf%d.128" % b] * (b < 2) + ["at"], ["zt%d" % b])
-        if k == 0:
-            scan(rr, ["rr%d" % k], "scr")
-            list_out(k)
-            tcopy(T.ir[:, 0:C].indirect(rt[:, 0:16]), T.wi[:, C:2 * C], ["wi", "rt%d" % k], ["ir"])
-            quant_z()
-            scan(T.ir, ["ir"], "sc2")
-        else:
-            tcopy(T.ir[:, 0:C].indirect(T.at[:, 0:16]), T.wi[:, C:2 * C], ["wi", "at"], ["ir"])
-            quant_z()
-            hop(T.iv, "iv", T.ir[:, 0:C], ["ir"], T["it%d" % (k - 1)], "it%d" % (k - 1), 0, 12)
-            scan(T.iv, ["iv.v", "iv.s"], "sc2")
+                if lo < 128 * h + 128 and hi > 128 * h:
+                    zw[h].append("zt%d.%d" % (b, lo))
+        for h in range(2):
+            c = 128 * h
+            quant(T.qz[:, c:c + 128], T.pz[:, c:c + 128], T.zt[:, 4 * c:4 * c + 512], zw[h], ["qz%d" % h])
+        n = OPT["iv"]
+        hop_s(T.iv, "iv", T.ir[:, 0:C], ["ir"], T[finv], finv, 0, n)
+        if n < 16:
+            hop_v(T.iv, "iv", T.ir[:, 0:C], ["ir"], T[finv], finv, 0, n)
+        early = OPT["rr"] in "DM"
+        r1, r2 = OPT["rcut"]
+        if early:
+            list_row(act, 0, r1, "a")
+            list_row(tcopy, r1, r2, "b")
+        scan(T.iv, ["iv.v", "iv.s"] if n < 16 else ["iv.s"], "sc2")
+        if early:
+            list_row(tcopy, r2, C, "c")
         table(it[:], 0.25, ["it%d" % k], "sc2")
-        cuts = ((0, 0, 128, T.psb[:, 0:128], "psb0"), (0, 128, C, T.psa[:, 0:128], "psa0")) + tuple(
-            (b, 0, C, T.psb[:, 512 * b:512 * b + C], "psb%d" % b) for b in (1, 2, 3))
+        if k < 2 and early:
+            scan(rr, ["rr%d%s" % (k, x) for x in "abc"], "scr")
+        cuts = ((0, 0, 128, T.psb[:, 0:128], "psb0"), (0, 128, C, T.psa[:, 0:128], "psa0"), (1, 0, C, T.psb[:, 512:512 + C], "psb1"),
+                (2, 0, C, T.psb[:, 1024:1024 + C], "psb2"), (3, 0, 128, T.psb[:, 1536:1664], "psb3"), (3, 128, C, T.psa[:, 512:640], "psa1"))
         for b, lo, hi, o, n in cuts:
-            mm(o, T.wq[:, 128 * b:128 * b + 128], T.wp[:, 128 * b:128 * b + 128], T.qz[:, lo:hi], T.pz[:, lo:hi], True, True,
+            mm(o, T.wq[:, 128 * b:128 * b + 128], T.wp[:, 128 * b:128 * b + 128], T.qz[:, lo:hi], T.pz[:, lo:hi],
                ["wq", "wp"] + ["qz%d" % h for h in range(2) if lo <= 128 * h < hi], [n])
         for b, lo, hi, o, n in cuts:
             act(T.pb[:, C * b + lo:C * b + hi], o, [n], ["pb%d.%d" % (b, lo)], 0.015625)
-        if k == 1:
-            list_row(rr, "rr1")
-        if k == 2:
-            list_row(T.lnf, "lnf")
         xn = T["xt%d" % (k + 1)]
-        for b, lo, hi in BACK[k == 2]:
-            ttt(xn[:, 4 * lo + b:4 * hi:4], T.pb[:, C * b:C * b + C].indirect(it[:, lo // 16:hi // 16]), T.fh[:, C * b + lo:C * b + hi], A.add,
-                ["pb%d.%d" % (c, l) for c, l, h, o, n in cuts if c == b] + ["it%d" % k, "fh%d" % b],
-                ["xt%d.%d.%d" % (k + 1, b, h) for h in range(2) if lo <= 128 * h < hi])
-    op("y", lambda: g.sync.dma_start(T.ln[:], T.lnf[0:128:16, :]), ["lnf"], ["ln"], "out", 16)
-    Q3 = ["qx3.0", "qx3.1"]
-    for h in range(2):
-        c = 128 * h
-        quant(T.qx3[:, c:c + 128], T.px3[:, c:c + 128], T.xt3[:, 4 * c:4 * c + 512], ["xt3.%d.%d" % (b, h) for b in range(4)], [Q3[h]])
-        mm(T.psa[:, 4 * c:4 * c + 128], T.vq[:, 0:128], T.vp[:, 0:128], T.qx3[:, c:c + 128], T.px3[:, c:c + 128], True, True, ["vq", Q3[h]], ["psa%d" % h])
-    op("y", lambda: g.sync.dma_start(T.oc[:, 0:4 * C], T.qx3[:, 0:C].bitcast(dt.uint8)), Q3, ["oc"], "out", 16)
-
-    def scales(q, queue, i):
-        op(q, lambda: queue.dma_start(T.osc[4 * i:4 * i + 4, 0:C], T.px3[32 * i:32 * i + 4, 0:C]), Q3, ["osc%d" % i], "out", 16)
-
-    scales("y", g.sync, 0)
-    scales("y", g.sync, 1)
-    tcopy(T.yb[:, 0:128], T.psa[:, 0:128], ["psa0"], ["y0"])
-    act(T.yb[:, 128:C], T.psa[:, 512:640], ["psa1"], ["y1"])
-    op("y", lambda: g.sync.dma_start(T.y[:, 0:128], T.yb[:, 0:128]), ["y0"], ["yo0"], "out", 16)
-    op("s", lambda: S.dma_start(T.y[:, 128:C], T.yb[:, 128:C]), ["y1"], ["yo1"], "out", 16)
-    scales("s", S, 2)
-    scales("s", S, 3)
+        Pb = [["pb%d.%d" % (c, l) for c, l, h, o, n in cuts if c == b] + ["it%d" % k] for b in range(4)]
+        Xn = [["xt%d.%d.%d" % (k + 1, b, h) for h in range(2)] for b in range(4)]
+        for what, b, lo, hi in OPT["back"][k == 2]:
+            hs = [h for h in range(2) if lo <= 128 * h < hi]
+            if what == "both":
+                ttt(xn[:, 4 * lo + b:4 * hi:4], T.pb[:, C * b:C * b + C].indirect(it[:, lo // 16:hi // 16]), T.fh[:, C * b + lo:C * b + hi], A.add,
+                    Pb[b] + ["fh%d.%d" % (b, 128 * h) for h in hs], [Xn[b][h] for h in hs])
+            if what == "pick":
+                act(T.pg[:, lo:hi], T.pb[:, b * C:b * C + C].indirect(it[:, lo // 16:hi // 16]), Pb[b], ["pg%d" % h for h in hs])
+            if what == "add":
+                ttt(xn[:, 4 * lo + b:4 * hi:4], T.psa[:, 512 * b + lo:512 * b + hi], T.pg[:, lo:hi], A.add, ["psa%d" % b] + ["pg%d" % h for h in hs], [Xn[b][h] for h in hs])
+            if what == "list" and k < 2:
+                list_out(k)
+            if what == "head" and k == 0 and lo == 0:
+                op("s", lambda: S.activation(T.c2[:], T.wi[:, 0:512].indirect(T.co[:, 0:16]), IDENTITY, bias=T.q2[:, 0:1], scale=2.0), ["wi", "co", "q2"], ["c2"])
+            if what == "head":
+                head(k + 1, hs[0])
+            if what == "store":
+                store(b, hs)
     for s, n in sorted(total.items()):
         g.wait_ge(T.sem[s], n)
-
-
-BACK = (((0, 0, C), (1, 0, C), (2, 0, C), (3, 0, C)), ((0, 0, C), (1, 0, C), (2, 0, C), (3, 0, C)))

from concourse.mybir import dt, AluOpType, ActivationFunctionType

C = 256
ROUNDS = (1, 2, 4)
COPY = ActivationFunctionType.Copy
IDENTITY = ActivationFunctionType.Identity
LIFT = 65536.0
CODES = "float8_e4m3fn_x4"
JUMPS = ((None, 2, 1, 1), (2, 3, 2, 1), (3, 5, 3, 2), (5, 8, 5, 3), (8, 13, 8, 5), (13, 21, 13, 8), (21, 34, 21, 13), (34, 55, 34, 21),
         (None, 89, 55, 34), (89, "A", 89, "e"), ("A", 178, 89, 89), (None, "a", 178, "A"))
MEETS = {"A": (0, 0, 128), 178: (0, 128, C), "a": (1, 0, 128)}
BACK = (("pick", 2, 0, 128), ("pick", 2, 128, C), ("both", 0, 0, C), ("list", 0, 0, 0), ("both", 1, 0, C), ("both", 3, 0, C), ("add", 2, 0, 128), ("add", 2, 128, C),
        ("head", 0, 0, 128), ("head", 0, 128, C))
LAST = BACK + (("store", "ln", 0, C), ("store", "oc", 0, C), ("store", "osc", 0, C), ("store", "yv", 0, 128), ("store", "ys", 128, C), ("store", "y", 0, C))
OPT = {"back": (BACK, LAST), "rr": "M", "sg": (2,), "lays": ((3, 2, 1, 0), ("e", 3, 2, 1)), "late": (("k0", "k1", "k3", "q"), ("k0", "k1", "k3", "q")), "fld": True, "n1": 12, "direct": (1, 2), "iv": 12, "rcut": (128, 192),
       "z": (("v", 0, 0, C), ("s", 1, 0, C), ("s", 2, 0, C), ("s", 3, 0, 128), ("s", 3, 128, C), ("v", None, 0, C))}

SCRATCH = {
    "fld": ("dram", [128, 16], "int32"), "flb": ("sbuf", [128, 16], "int32"), "ft": ("sbuf", [128, 16], "uint16"), "fi": ("sbuf", [128, 16], "uint16"), "fr": ("sbuf", [128, C], "bfloat16"),
    "ut": ("sbuf", [128, 512], "bfloat16"), "uq": ("sbuf", [128, 128], CODES), "up": ("sbuf", [128, 128], "uint8"),
    "urq": ("sbuf", [128, 128], CODES), "urp": ("sbuf", [128, 128], "uint8"),
    "vt": ("sbuf", [128, 512], "bfloat16"), "vq": ("sbuf", [128, 128], CODES), "vp": ("sbuf", [128, 128], "uint8"),
    "wq": ("sbuf", [128, 512], CODES), "wp": ("sbuf", [128, 512], "uint8"),
    "ew": ("sbuf", [128, 516], "bfloat16"), "eq": ("sbuf", [128, 512], CODES), "ep": ("sbuf", [128, 512], "uint8"),
    "zt": ("sbuf", [128, 1024], "bfloat16"), "qz": ("sbuf", [128, C], CODES), "pz": ("sbuf", [128, C], "uint8"),
    "fh": ("sbuf", [128, 1024], "bfloat16"), "zf": ("sbuf", [128, 1024], "bfloat16"),
    "xf": ("sbuf", [128, 1024], "bfloat16"), "qf": ("sbuf", [128, C], CODES), "pf": ("sbuf", [128, C], "uint8"),
    "f4": ("sbuf", [128, 64], "uint16"),
    "pb": ("sbuf", [128, 1024], "float32"), "pg": ("sbuf", [128, C], "float32"),
    "wi": ("sbuf", [128, 516], "bfloat16"), "wcol": ("sbuf", [128, 1], "float32"),
    "jm": ("sbuf", [128, 16], "int32"), "jm2": ("sbuf", [128, 16], "int32"), "r16": ("sbuf", [128, 16], "float32"),
    "k16": ("sbuf", [128, 16], "float32"), "c16": ("sbuf", [128, 16], "float32"), "po": ("sbuf", [128, 16], "uint16"),
    "thr": ("sbuf", [128, C], "float32"), "cu": ("sbuf", [128, C], "bfloat16"), "rst": ("sbuf", [128, C], "bfloat16"),
    "sc0": ("sbuf", [128, 1], "float32"), "scc": ("sbuf", [128, 1], "float32"),
    "pq": ("sbuf", [128, 16], "int32"), "pq2": ("sbuf", [128, 16], "int32"), "cj": ("sbuf", [128, 16], "float32"),
    "jj": ("sbuf", [128, 16], "float32"), "jh": ("sbuf", [128, 16], "float32"),
    "oi": ("sbuf", [128, 8], "int32"), "ou": ("sbuf", [128, 8], "uint16"),
    "mb": ("sbuf", [128, C], "bfloat16"), "ms": ("sbuf", [128, C], "bfloat16"),
    "sc1": ("sbuf", [128, C], "bfloat16"), "sc2": ("sbuf", [128, C], "bfloat16"), "scr": ("sbuf", [128, C], "bfloat16"),
    "eh": ("sbuf", [128, 16], "float32"), "ed": ("sbuf", [128, 16], "float32"),
    "pk": ("sbuf", [128, 48], "float32"), "ts": ("sbuf", [128, 64], "float32"),
    "d0": ("sbuf", [128, 64], "float32"), "d1": ("sbuf", [128, 64], "float32"), "sb": ("sbuf", [128, 16], "float32"), "ch": ("sbuf", [128, 16], "float32"),
    "co": ("sbuf", [128, 16], "uint16"), "q2": ("sbuf", [128, 1], "float32"), "c2": ("sbuf", [128, C], "bfloat16"),
    "ea": ("sbuf", [128, 512], "bfloat16"), "eb": ("sbuf", [128, 512], "bfloat16"), "wd": ("sbuf", [128, 512], "bfloat16"),
    "tt": ("sbuf", [128, 16 * 12], "uint16"),
    "w0": ("sbuf", [128, 512], "bfloat16"), "w1": ("sbuf", [128, 512], "bfloat16"), "w2": ("sbuf", [128, 512], "bfloat16"),
    "aa": ("sbuf", [128, C], "bfloat16"), "ar": ("sbuf", [128, C], "bfloat16"), "at": ("sbuf", [128, 16], "uint16"),
    "ir": ("sbuf", [128, C], "bfloat16"), "iv": ("sbuf", [128, C], "bfloat16"),
    "lnf": ("sbuf", [128, C], "float32"), "yb": ("sbuf", [128, C], "float32"),
    "psa": ("psum", [128, 2048], "float32"), "psb": ("psum", [128, 2048], "float32"),
    "el0": ("sbuf", [128, 16], "int32"), "el1": ("sbuf", [128, 16], "uint16"), "el2": ("sbuf", [128, 16], "uint16"),
}
for _k in range(4):
    SCRATCH["xt%d" % _k] = ("sbuf", [128, 1024], "bfloat16")
    SCRATCH["qx%d" % _k] = ("sbuf", [128, C], CODES)
    SCRATCH["px%d" % _k] = ("sbuf", [128, C], "uint8")
for _k in range(3):
    SCRATCH["lq%d" % _k] = ("sbuf", [128, C], CODES)
    SCRATCH["lp%d" % _k] = ("sbuf", [128, C], "uint8")
    SCRATCH["st%d" % _k] = ("sbuf", [128, 48], "bfloat16")
    SCRATCH["sl%d" % _k] = ("sbuf", [128, 48], "bfloat16")
    SCRATCH["su%d" % _k] = ("sbuf", [128, 16], "uint16")
    SCRATCH["sv%d" % _k] = ("sbuf", [128, 16], "uint16")
    SCRATCH["rr%d" % _k] = ("sbuf", [128, C], "bfloat16")
    SCRATCH["rt%d" % _k] = ("sbuf", [128, 16], "uint16")
    SCRATCH["it%d" % _k] = ("sbuf", [128, 16], "uint16")
SEMAPHORES = (["cv", "cs", "cp", "cg", "lo", "ld", "lf", "lx", "lu", "lv", "lw", "lws", "out"]
              + ["%s%d" % (a, k) for a in ("ar_s", "ar_l", "ar_d") for k in range(3)])


def rank_program(g, core, T, topo):
    rank = T.rank_of(core)
    if rank is None:
        return
    V, S, P = g.vector, g.scalar, g.tensor
    queues = {"v": V, "s": S, "p": P, "g": g, "y": g.sync}
    own = {"v": "cv", "s": "cs", "p": "cp", "g": "cg"}
    known = {q: {} for q in queues}
    snap = {}
    total = {}
    wrote, read = {}, {}

    def covered(k, d):
        return k.get(d[0], 0) >= d[1]

    def wait(q, deps):
        best = {}
        for d in deps:
            if not covered(known[q], d):
                best[d[0]] = max(best.get(d[0], 0), d[1])
        deps = list(best.items())
        for d in deps:
            if any(o != d and covered(snap[o], d) for o in deps):
                continue
            queues[q].wait_ge(T.sem[d[0]], d[1])
        for d in deps:
            known[q][d[0]] = max(known[q].get(d[0], 0), d[1])
            for s, n in snap[d].items():
                known[q][s] = max(known[q].get(s, 0), n)

    def needs(reads, writes):
        deps = [wrote[t] for t in reads]
        for t in writes:
            if t in wrote:
                deps.append(wrote[t])
            deps += read.get(t, [])
        return deps

    def op(q, call, reads, writes, sem=None, inc=1):
        wait(q, needs(reads, writes))
        name = sem or own[q]
        ins = call()
        ins.then_inc(T.sem[name], inc)
        total[name] = total.get(name, 0) + inc
        me = (name, total[name])
        snap[me] = dict(known[q])
        for t in reads:
            read.setdefault(t, []).append(me)
        for t in writes:
            wrote[t], read[t] = me, []

    def arrives(sem, n, tokens):
        total[sem] = total.get(sem, 0) + n
        for t in tokens:
            wrote[t] = (sem, total[sem])
        snap[(sem, total[sem])] = {}

    def send(dst, out, in_, sem, reads):
        wait("g", needs(reads, []))
        rid, pid, _ = topo.addr(dst)
        g.remote_dma(out, in_, T.sem[sem], T.sem.lo, pid, rid, topo.mask(core, dst))
        total["lo"] = total.get("lo", 0) + len(topo.engines(core, dst))

    def tcopy(out, in_, r, w):
        op("v", lambda: V.tensor_copy(out, in_), r, w)

    def tts(out, in0, s1, s2, o0, o1, r, w):
        if o1 is None:
            op("v", lambda: V.tensor_scalar(out, in0, s1, None, o0), r, w)
        else:
            op("v", lambda: V.tensor_scalar(out, in0, s1, s2, o0, o1), r, w)

    def ttt(out, a, b, o, r, w):
        op("v", lambda: V.tensor_tensor(out, a, b, o), r, w)

    def fill(ap, value, w):
        op("v", lambda: V.memset(ap, value), [], w)

    def quant(q, p, t, r, w):
        op("v", lambda: V.quantize_mx(q, p, t), r, w)

    def act(out, in_, r, w, scale=None):
        if scale is None:
            op("s", lambda: S.activation(out, in_, COPY), r, w)
        else:
            op("s", lambda: S.activation(out, in_, COPY, scale=scale), r, w)

    def mm(out, a, ap, b, bp, r, w, start=True, stop=True):
        op("p", lambda: P.matmul_mx(out, a, ap, b, bp, start, stop), r, w)

    def iota(out, pattern, base, cm, w, small=False):
        if small:
            op("g", lambda: g.iota(out, pattern, base, cm, allow_small_or_imprecise_dtypes=True), [], w)
        else:
            op("g", lambda: g.iota(out, pattern, base, cm), [], w)

    A = AluOpType

    def scan(row, r, w):
        op("v", lambda: V.tensor_tensor_scan(T[w][:, 0:C], T.cu[:, 0:C], row[:, 0:C], 0.0, A.mult, A.add), r + ["cu"], [w])

    def table(out, bias, w, s):
        tts(out, T[s][:, 15:C:16], T.scc[:, 0:1], bias, A.mult, A.add, [s, "scc"], w)

    def hop_s(out, w, window, reads, off, oname, c0, n):
        act(out[:, 0:16 * n], window.indirect(off[:, c0:c0 + n]), reads + [oname], [w + ".s"])

    def hop_v(out, w, window, reads, off, oname, c0, n):
        tcopy(out[:, 16 * n:C], window.indirect(off[:, c0 + n:c0 + 16]), reads + [oname], [w + ".v"])

    def hop(*a):
        hop_s(*a)
        hop_v(*a)

    if OPT["fld"]:
        op("s", lambda: S.dma_start(T.fld[:], T.fl[:]), [], ["fld"], "ld", 16)
    else:
        op("s", lambda: S.dma_start(T.flb[:], T.fl[:]), [], ["flb"], "lf", 16)
    op("y", lambda: g.sync.dma_start(T.ut[:], T.u[:]), [], ["ut"], "lu", 16)
    op("y", lambda: g.sync.dma_start(T.xt0[:], T.x[:]), [], ["xt0.%d.%d" % (b, h) for b in range(4) for h in range(2)], "lx", 16)
    if OPT["fld"]:
        op("y", lambda: g.sync.dma_start(T.flb[:], T.fl[:]), [], ["flb"], "lf", 16)
    iota(T.jm[:], [[1, 16]], 0, -1, ["jm"])
    iota(T.pq[:], [[0, 16]], 0, 1, ["pq"])
    iota(T.wcol[:], [[0, 1]], 3 - C, 4, ["wcol"], True)
    iota(T.wi[:], [[1, 516]], -C, 0, ["wi"], True)
    iota(T.oi[:], [[16, 8]], 0, 0, ["oi"])
    iota(T.cj[:], [[16, 16]], C, 0, ["cj"], True)
    first = T.cores[rank ^ ROUNDS[0]]
    if OPT["fld"]:
        send(first, T.el0[:], T.fld[:], "ar_l0", ["fld"])
    else:
        send(first, T.el0[:], T.flb[:], "ar_l0", ["flb"])
    arrives("ar_l0", len(topo.engines(first, core)), ["el0"])
    fill(T.st0[:], -1.0, ["st0"])
    fill(T.d0[:], -1.0, ["d0"])
    iota(T.w0[:, C:2 * C], [[1, C]], 0, 0, ["w0.k"], True)
    tts(T.jm2[:], T.jm[:], 15, None, A.bitwise_and, None, ["jm"], ["jm2"])
    tts(T.pq2[:], T.pq[:], 15, None, A.bitwise_and, None, ["pq"], ["pq2"])
    fill(T.st0[:, 0:48:3], 0.0, ["st0"])
    fill(T.d0[:, 0:64:4], 0.0, ["d0"])
    tts(T.r16[:], T.jm2[:], 0.0, None, A.not_equal, None, ["jm2"], ["r16"])
    tts(T.k16[:], T.jm2[:], 1.0, LIFT - 1.0, A.is_equal, A.mult, ["jm2"], ["k16"])
    tcopy(T.po[:], T.pq2[:], ["pq2"], ["po"])
    tts(T.sc0[:], T.jm2[:, 15:16], 0.0, 1.0 - 1.0 / LIFT, A.is_equal, A.mult, ["jm2"], ["sc0"])
    ttt(T.c16[:], T.k16[:], T.r16[:], A.add, ["k16", "r16"], ["c16"])
    tts(T.scc[:], T.sc0[:], 1.0 / LIFT, None, A.add, None, ["sc0"], ["scc"])
    act(T.rst[:], T.r16[:, 0:16].indirect(T.po[:, 0:16]), ["r16", "po"], ["rst"])
    act(T.cu[:], T.c16[:, 0:16].indirect(T.po[:, 0:16]), ["c16", "po"], ["cu"])
    act(T.thr[:], T.rst[:], ["rst"], ["thr"], 1.0e29)
    tts(T.ew[:], T.wi[:], T.wcol[:, 0:1], 0.5, A.is_equal, A.mult, ["wi", "wcol"], ["ew"])

    def own_list():
        tcopy(T.ft[:], T.flb[:], ["flb"], ["ft"])

    def own_row():
        act(T.fr[:], T.wi[:, C:2 * C].indirect(T.ft[:, 0:16]), ["wi", "ft"], ["fr"])

    if not OPT["fld"]:
        own_list()

    def quant_e(b):
        quant(T.eq[:, 128 * b:128 * b + 128], T.ep[:, 128 * b:128 * b + 128], T.ew[:, 3 - b:515 - b], ["ew"], ["eq%d" % b])

    def four(name, b):
        tts(T.f4[:, 16 * b:16 * b + 16], T[name][:], 4.0, float(b), A.mult, A.add, [name], ["f4.%d" % b])

    tcopy(T.ou[:], T.oi[:], ["oi"], ["ou"])
    ttt(T.jj[:], T.pq2[:], T.cj[:], A.add, ["pq2", "cj"], ["jj"])
    quant_e(0)
    tts(T.jh[:], T.jj[:], 0.5, None, A.mult, None, ["jj"], ["jh"])
    quant_e(1)
    quant(T.uq[:, 0:128], T.up[:, 0:128], T.ut[:, 0:512], ["ut"], ["uq"])
    quant_e(2)
    op("v", lambda: V.tensor_copy(T.urq[:, 0:128].bitcast(dt.uint32), T.uq[:, 0:128].bitcast(dt.uint32).indirect(T.ou[:, 0:8])), ["uq", "ou"], ["urq"])
    act(T.urp[:, 0:128], T.up[:, 0:128].indirect(T.ou[:, 0:8]), ["uq", "ou"], ["urp"])
    if not OPT["fld"]:
        own_row()
        for b in (3, 2, 1, 0):
            four("flb", b)
    else:
        quant_e(3)
    laid_by = []
    consts = {21: lambda: (fill(T.d0[:, 1:64:4], 4.0, ["d0"]), tts(T.q2[:], T.pq2[:, 0:1], 2.0, None, A.mult, None, ["pq2"], ["q2"])),
              34: lambda: (tts(T.co[:], T.cj[:], -128.0, None, A.add, None, ["cj"], ["co"]), tts(T.ch[:], T.jj[:], 2.0, 0.5 - 3 * C, A.mult, A.add, ["jj"], ["ch"])),
              55: lambda: tts(T.d1[:, 1:64:4], T.jj[:], -8.0, 8.0 * C - 2.0, A.mult, A.add, ["jj"], ["d1.1"])}

    def head(k, h):
        c = 128 * h
        q, p, name = T["qx%d" % k], T["px%d" % k], "qx%d.%d" % (k, h)
        quant(q[:, c:c + 128], p[:, c:c + 128], T["xt%d" % k][:, 4 * c:4 * c + 512], ["xt%d.%d.%d" % (k, b, h) for b in range(4)], [name])
        a, ap, r = (T.urq, T.urp, ["urq", "urp"]) if k < 3 else (T.vq, T.vp, ["vq"])
        mm(T.psb[:, 4 * c:4 * c + 128], a[:, 0:128], ap[:, 0:128], q[:, c:c + 128], p[:, c:c + 128], r + [name], ["psb%d" % h])

    def store(what, hs):
        lo, hi = 128 * hs[0], 128 * hs[-1] + 128
        Q3 = ["qx3.%d" % h for h in hs]
        if what == "ln":
            act(T.lnf[:], T.rr1[:, 0:C].indirect(T.at[:, 0:16]), ["rr1a", "rr1b", "rr1c", "at"], ["lnf"])
            op("y", lambda: g.sync.dma_start(T.ln[:], T.lnf[0:128:16, :]), ["lnf"], ["ln"], "out", 16)
        if what == "oc":
            op("y", lambda: g.sync.dma_start(T.oc[:, 4 * lo:4 * hi], T.qx3[:, lo:hi].bitcast(dt.uint8)), Q3, ["oc%d" % lo], "out", 16)
        if what == "osc":
            for i in range(4):
                op("y", lambda i=i: g.sync.dma_start(T.osc[4 * i:4 * i + 4, 0:C], T.px3[32 * i:32 * i + 4, 0:C]), Q3, ["osc%d" % i], "out", 16)
        if what in ("yv", "ys"):
            (tcopy if what == "yv" else act)(T.yb[:, lo:hi], T.psb[:, 4 * lo:4 * lo + 128], ["psb%d" % hs[0]], ["y%d" % hs[0]])
        if what == "y":
            op("s", lambda: S.dma_start(T.y[:, lo:hi], T.yb[:, lo:hi]), ["y%d" % h for h in hs], ["yo%d" % lo], "out", 16)

    head(0, 0)
    head(0, 1)

    for k, m in enumerate(ROUNDS):
        d = T.cores[rank ^ m]
        ne = len(topo.engines(d, core))
        xt, qx, px = T["xt%d" % k], T["qx%d" % k], T["px%d" % k]
        lq, lp, st, sl, el = T["lq%d" % k], T["lp%d" % k], T["st%d" % k], T["sl%d" % k], T["el%d" % k]
        rr, rt, it = T["rr%d" % k], T["rt%d" % k], T["it%d" % k]
        Xt = ["xt%d.%d.%d" % (k, b, h) for b in range(4) for h in range(2)]
        Qx = ["qx%d.0" % k, "qx%d.1" % k]
        frow, ftab, finv = ("fr", "ft", "fi") if k == 0 else ("rr%d" % (k - 1), "rt%d" % (k - 1), "it%d" % (k - 1))
        Fr = ["fr"] if k == 0 else [frow + x for x in "abc"]

        def unpack(ps, name, q, p, r, start=True, stop=True):
            for b in range(4):
                mm(ps[:, 512 * b:512 * b + C], T.eq[:, 128 * b:128 * b + 128], T.ep[:, 128 * b:128 * b + 128], q[:, 0:C], p[:, 0:C], ["eq%d" % b] + r, [name + str(b)],
                   start, stop)

        def keep(b, lo, hi):
            act(T.fh[:, C * b + lo:C * b + hi], T.psa[:, 512 * b + lo:512 * b + hi], ["psa%d" % b], ["fh%d.%d" % (b, c) for c in (0, 128) if lo <= c < hi])

        def lay(f, b):
            f(T.xf[:, b:1024:4], xt[:, 0:1024].indirect(T.f4[:, 16 * b:16 * b + 16]), Xt + ["f4.%d" % b], ["xf%d" % b])

        def quant_f(h):
            c = 128 * h
            quant(T.qf[:, c:c + 128], T.pf[:, c:c + 128], T.xf[:, 4 * c:4 * c + 512], ["xf%d" % b for b in range(4)], ["qf%d" % h])

        def list_out(k):
            table(T["rt%d" % k][:], 0.25, ["rt%d" % k], "scr")
            nd = T.cores[rank ^ ROUNDS[k + 1]]
            send(nd, T["el%d" % (k + 1)][:], T["rt%d" % k][:], "ar_l%d" % (k + 1), ["rt%d" % k])
            arrives("ar_l%d" % (k + 1), len(topo.engines(nd, core)), ["el%d" % (k + 1)])

        if k == 0:
            gaps = [[lambda: quant_e(3)], [], [], [], []]
            if OPT["fld"]:
                gaps = [[lambda b=b: four("flb", b) for b in (3, 2, 1, 0)], [], [own_list], [], []]
        elif OPT["rr"] == "D":
            gaps = [[lambda b=b: four(ftab, b) for b in (1, 0)], [], [], [], []]
        elif OPT["rr"] == "M":
            gaps = [[lambda b=b: four(ftab, b) for b in (3, 2, 1, 0)], [], [], [], []]
        else:
            gaps = [[lambda: scan(T[frow], Fr, "scr")], [lambda: list_out(k - 1)], [lambda: four(ftab, 3)], [lambda: four(ftab, 2), lambda: four(ftab, 1)], [lambda: four(ftab, 0)]]
        laid = []
        direct = k in OPT["direct"]
        if direct:
            st, sl = T["su%d" % k], T["sv%d" % k]

        def gap(i):
            for f in gaps[i]:
                f()
            for b in OPT["lays"][k > 0]:
                if b == "e":
                    if b not in laid and direct:
                        act(T.ea[:, 0:512:2], T.wi[:, 0:C].indirect(el[:, 0:16]), ["wi", "el%d" % k], ["ea.e"])
                        laid.append(b)
                elif b not in laid and wrote["f4.%d" % b] not in laid_by:
                    lay(act, b)
                    laid.append(b)
                    laid_by.append(wrote["f4.%d" % b])

        gap(0)
        for h in range(2):
            c = 128 * h
            ttt(T.mb[:, c:c + 128], T.psb[:, 4 * c:4 * c + 128], T.thr[:, c:c + 128], A.is_gt, ["psb%d" % h, "thr"], ["mb%d" % h])
            if h == 0:
                gap(1)
        for h in range(2):
            c = 128 * h
            if direct:
                op("v", lambda: V.tensor_tensor_scan(T.ms[:, c:c + 128], T.c2[:, c:c + 128], T.mb[:, c:c + 128], -1000.0, A.max, A.add), ["c2", "mb%d" % h], ["ms%d" % h])
            else:
                op("v", lambda: V.tensor_tensor_scan(T.ms[:, c:c + 128], T.rst[:, c:c + 128], T.mb[:, c:c + 128], 0.0, A.mult, A.add), ["rst", "mb%d" % h], ["ms%d" % h])
            gap(2 + h)
        if direct:
            tts(st[:], T.ms[:, 15:C:16], float(C), None, A.add, None, ["ms0", "ms1"], ["st%d" % k])
        else:
            tts(st[:, 1:48:3], T.ms[:, 15:C:16], 2.0, -1.0, A.mult, A.add, ["ms0", "ms1"], ["st%d" % k])
        send(d, sl[:], st[:], "ar_s%d" % k, ["st%d" % k])
        arrives("ar_s%d" % k, ne, ["sl%d" % k])
        send(d, lq[:, 0:C].bitcast(dt.uint8), qx[:, 0:C].bitcast(dt.uint8), "ar_d%d" % k, Qx)
        send(d, lp[:, 0:C], px[:, 0:C], "ar_d%d" % k, Qx)
        arrives("ar_d%d" % k, 2 * ne, ["lq%d" % k])
        if k == 0:
            wait("y", [wrote["sl0"]])
            op("y", lambda: g.sync.dma_start(T.wq[:, 0:512].bitcast(dt.uint8), T.wc[:]), [], ["wq"], "lw", 16)
            op("y", lambda: g.sync.dma_start(T.wp[:, 0:512], T.ws[:]), [], ["wp"], "lws", 16)
            op("y", lambda: g.sync.dma_start(T.vt[:], T.v[:]), [], ["vt"], "lv", 16)
        gap(4)
        unpack(T.psa, "psa", qx, px, Qx)
        if k == 0:
            for n in ("w1", "w2"):
                iota(T[n][:, C:2 * C], [[1, C]], 0, 0, [n + ".k"], True)
            iota(T.ea[:, 1:512:2], [[1, C]], 0, 0, ["ea.k"], True)
            iota(T.eb[:, 0:512:2], [[1, C]], 0, 0, ["eb.k"], True)
        if direct:
            ttt(T.sb[:], T.ms[:, 15:C:16], T.ch[:], A.subtract, ["ms0", "ms1", "ch"], ["sb"])
            tts(T.eh[:], el[:], 0.5, None, A.mult, None, ["el%d" % k], ["eh"])
            tcopy(T.eb[:, 1:512:2], T.ea[:, 0:512:2], ["ea.e"], ["eb.e"])
            ttt(T.ed[:], T.eh[:], T.jh[:], A.subtract, ["eh", "jh"], ["ed"])
            ttt(T.d1[:, 2:64:4], T.eh[:], T.jh[:], A.add, ["eh", "jh"], ["d1.2"])
            tcopy(T.wd[:, 0:512:2], T.ea[:, 0:512].indirect(st[:, 0:16]), ["ea.e", "ea.k", "st%d" % k], ["wd0"])
            act(T.wd[:, 1:512:2], T.eb[:, 0:512].indirect(st[:, 0:16]), ["eb.e", "eb.k", "st%d" % k], ["wd1"])
            ttt(T.d0[:, 2:64:4], T.ed[:], T.sb[:], A.mult, ["ed", "sb", "d0"], ["d0.2"])
            tts(T.d1[:, 3:64:4], T.d1[:, 2:64:4], 2.0, None, A.mult, None, ["d1.2"], ["d1.3"])
        for b in range(4):
            if b not in laid:
                lay(tcopy, b)
                laid_by.append(wrote["f4.%d" % b])
        late = OPT["late"][k > 0]
        late_s, late_v = [], []
        if k == 0 and OPT["fld"]:
            own_row()
        for b in range(4):
            if b not in OPT["sg"]:
                if "k%d" % b not in late:
                    keep(b, 0, C)
                else:
                    late_s += [lambda b=b: keep(b, 0, 128), lambda b=b: keep(b, 128, C)]

        def meet_products():
            unpack(T.psb, "psb", T.qf, T.pf, ["qf0", "qf1"], True, False)
            unpack(T.psb, "psb", lq, lp, ["lq%d" % k], False, True)

        if direct:
            if "q" not in late:
                quant_f(0)
                quant_f(1)
            else:
                late_v += [lambda: quant_f(0), lambda: (quant_f(1), meet_products())]
        else:
            tts(T.eh[:], el[:], 0.5, None, A.mult, None, ["el%d" % k], ["eh"])
            if k == 0:
                tcopy(T.ir[:, 0:C].indirect(T.ft[:, 0:8]), T.wi[:, C:C + 128], ["wi", "ft"], ["ir"])
            if "q" not in late:
                quant_f(0)
            ttt(T.ed[:], T.eh[:], T.jh[:], A.subtract, ["eh", "jh"], ["ed"])
            ttt(T.pk[:, 1:48:3], T.eh[:], T.jh[:], A.add, ["eh", "jh"], ["pk1"])
            if k == 0:
                tcopy(T.ir[:, 0:C].indirect(T.ft[:, 8:16]), T.wi[:, C + 128:2 * C], ["wi", "ft"], ["ir"])
            if "q" not in late:
                quant_f(1)
            else:
                late_v += [lambda: quant_f(0), lambda: (quant_f(1), meet_products())]
            ttt(T.pk[:, 0:48:3], T.ed[:], st[:, 1:48:3], A.mult, ["ed", "st%d" % k], ["pk0"])
            tts(T.pk[:, 2:48:3], T.pk[:, 1:48:3], 2.0, None, A.mult, None, ["pk1"], ["pk2"])
        if not late_v:
            meet_products()

        def meet(f, b, lo, hi):
            f(T.zf[:, C * b + lo:C * b + hi], T.psb[:, 512 * b + lo:512 * b + hi], ["psb%d" % b], ["zf%d.%d" % (b, c) for c in (0, 128) if lo <= c < hi])

        tabs = {1: 0, "e": 16}
        rows = {1: "w0", "A": "aa", "a": "ar"}
        if direct:
            args = (T.w0, "w0", T.wd[:, 0:512], ["wd0", "wd1"], sl, "sl%d" % k, 0, OPT["n1"])
            hop_s(*args)
            tcopy(T.d1[:, 0:64:4], sl[:], ["sl%d" % k], ["d1.0"])
            if OPT["n1"] < 16:
                hop_v(*args)
            else:
                wrote["w0.v"] = wrote["w0.s"]
            op("v", lambda: V.tensor_tensor_scan(T.ts[:], T.d0[:], T.d1[:], 0.0, A.mult, A.add), ["d0", "d0.2"] + ["d1.%d" % i for i in range(4)], ["ts"])
            tcopy(T.tt[:, 0:16], T.ts[:, 2:64:4], ["ts"], ["tt1"])
            tcopy(T.tt[:, 16:32], T.ts[:, 3:64:4], ["ts"], ["tte"])
        else:
            op("v", lambda: V.tensor_tensor_scan(T.ts[:, 0:48], sl[:], T.pk[:], 0.0, A.mult, A.add), ["sl%d" % k, "pk0", "pk1", "pk2"], ["ts"])
            tcopy(T.tt[:, 0:16], T.ts[:, 1:48:3], ["ts"], ["tt1"])
            hop(T.w0, "w0", T.wi[:, 0:512], ["wi"], T.tt, "tt1", 0, 8)
            tcopy(T.tt[:, 16:32], T.ts[:, 2:48:3], ["ts"], ["tte"])
        for i, (tab, new, win, by) in enumerate(JUMPS):
            if new not in rows:
                rows[new] = "w%d" % ((len(rows) - 2) % 3)
            w, o = rows[win], rows[new]
            args = (T[o], o, T[w][:, 0:512], [w + ".v", w + ".s", w + ".k"], T.tt, "tt%s" % by, tabs[by], 8 if tab is None else 10)
            hop_s(*args)
            if tab is not None:
                scan(T[rows[tab]], [rows[tab] + ".v", rows[tab] + ".s"], "sc%d" % (1 + i % 2))
            hop_v(*args)
            if tab is not None:
                tabs[tab] = 16 * len(tabs)
                table(T.tt[:, tabs[tab]:tabs[tab] + 16], 256.25, ["tt%s" % tab], "sc%d" % (1 + i % 2))
            if late_s and tab is not None:
                late_s.pop(0)()
            if late_v and tab is not None:
                late_v.pop(0)()
            if k == 0 and new in consts:
                consts[new]()
            if k == 0 and new == 8:
                scan(T.ir, ["ir"], "scr")
            if k == 0 and new == 13:
                table(T.fi[:], 0.25, ["fi"], "scr")
            if k == 1 and new == 13:
                quant(T.vq[:, 0:128], T.vp[:, 0:128], T.vt[:, 0:512], ["vt"], ["vq"])
            if new in MEETS:
                meet(tcopy, *MEETS[new])
        meet(act, 2, 0, C)
        meet(act, 3, 0, C)
        scan(T.ar, ["ar.v", "ar.s"], "sc1")
        meet(tcopy, 1, 128, C)
        table(T.at[:], 0.25, ["at"], "sc1")

        def list_row(f, lo, hi, name):
            if k < 2:
                f(rr[:, lo:hi], T[frow][:, 0:C].indirect(T.at[:, lo // 16:hi // 16]), Fr + ["at"], ["rr%d%s" % (k, name)])

        zw = [[], []]
        for i, (e, b, lo, hi) in enumerate(OPT["z"]):
            if b is None:
                tcopy(T.ir[:, 0:C].indirect(T.at[:, lo // 16:hi // 16]), T.wi[:, C + lo:C + hi], ["wi", "at"], ["ir"])
                continue
            (tcopy if e == "v" else act)(T.zt[:, 4 * lo + b:4 * hi:4], T.zf[:, C * b:C * b + C].indirect(T.at[:, lo // 16:hi // 16]),
                                         ["zf%d.0" % b, "zf%d.128" % b, "at", "qzr"][:3], ["zt%d.%d" % (b, lo)])
            for h in range(2):
                if lo < 128 * h + 128 and hi > 128 * h:
                    zw[h].append("zt%d.%d" % (b, lo))
        for h in range(2):
            c = 128 * h
            quant(T.qz[:, c:c + 128], T.pz[:, c:c + 128], T.zt[:, 4 * c:4 * c + 512], zw[h], ["qz%d" % h])
        n = OPT["iv"]
        hop_s(T.iv, "iv", T.ir[:, 0:C], ["ir"], T[finv], finv, 0, n)
        if n < 16:
            hop_v(T.iv, "iv", T.ir[:, 0:C], ["ir"], T[finv], finv, 0, n)
        early = OPT["rr"] in "DM"
        r1, r2 = OPT["rcut"]
        if early:
            list_row(act, 0, r1, "a")
            list_row(tcopy, r1, r2, "b")
        scan(T.iv, ["iv.v", "iv.s"] if n < 16 else ["iv.s"], "sc2")
        if early:
            list_row(tcopy, r2, C, "c")
        table(it[:], 0.25, ["it%d" % k], "sc2")
        if k < 2 and early:
            scan(rr, ["rr%d%s" % (k, x) for x in "abc"], "scr")
        cuts = ((0, 0, 128, T.psb[:, 0:128], "psb0"), (0, 128, C, T.psa[:, 0:128], "psa0"), (1, 0, C, T.psb[:, 512:512 + C], "psb1"),
                (2, 0, C, T.psb[:, 1024:1024 + C], "psb2"), (3, 0, 128, T.psb[:, 1536:1664], "psb3"), (3, 128, C, T.psa[:, 512:640], "psa1"))
        for b, lo, hi, o, n in cuts:
            mm(o, T.wq[:, 128 * b:128 * b + 128], T.wp[:, 128 * b:128 * b + 128], T.qz[:, lo:hi], T.pz[:, lo:hi],
               ["wq", "wp"] + ["qz%d" % h for h in range(2) if lo <= 128 * h < hi], [n])
        for b, lo, hi, o, n in cuts:
            act(T.pb[:, C * b + lo:C * b + hi], o, [n], ["pb%d.%d" % (b, lo)], 0.015625)
        xn = T["xt%d" % (k + 1)]
        Pb = [["pb%d.%d" % (c, l) for c, l, h, o, n in cuts if c == b] + ["it%d" % k] for b in range(4)]
        Xn = [["xt%d.%d.%d" % (k + 1, b, h) for h in range(2)] for b in range(4)]
        for what, b, lo, hi in OPT["back"][k == 2]:
            hs = [h for h in range(2) if lo <= 128 * h < hi]
            if what == "both":
                ttt(xn[:, 4 * lo + b:4 * hi:4], T.pb[:, C * b:C * b + C].indirect(it[:, lo // 16:hi // 16]), T.fh[:, C * b + lo:C * b + hi], A.add,
                    Pb[b] + ["fh%d.%d" % (b, 128 * h) for h in hs], [Xn[b][h] for h in hs])
            if what == "pick":
                act(T.pg[:, lo:hi], T.pb[:, b * C:b * C + C].indirect(it[:, lo // 16:hi // 16]), Pb[b], ["pg%d" % h for h in hs])
            if what == "add":
                ttt(xn[:, 4 * lo + b:4 * hi:4], T.psa[:, 512 * b + lo:512 * b + hi], T.pg[:, lo:hi], A.add, ["psa%d" % b] + ["pg%d" % h for h in hs], [Xn[b][h] for h in hs])
            if what == "list" and k < 2:
                list_out(k)
            if what == "head" and k == 0 and lo == 0:
                op("s", lambda: S.activation(T.c2[:], T.wi[:, 0:512].indirect(T.co[:, 0:16]), IDENTITY, bias=T.q2[:, 0:1], scale=2.0), ["wi", "co", "q2"], ["c2"])
            if what == "head":
                head(k + 1, hs[0])
            if what == "store":
                store(b, hs)
    for s, n in sorted(total.items()):
        g.wait_ge(T.sem[s], n)
